import numpy as np, ml_dtypes
CORES = [25,29,65,69,153,157,193,197]
N = 8
import mx_ref
BF = ml_dtypes.bfloat16
def gentries(a):
    return np.ascontiguousarray(a.reshape(8, 16, -1).transpose(0, 2, 1)).reshape(8, -1)
def gtable(e):
    e = np.asarray(e); return np.ascontiguousarray(e.reshape(8, -1, 16).transpose(0, 2, 1)).reshape(128, -1).astype(np.int32)
def gcols(t, e):
    v = np.concatenate([t.reshape(8, 16, -1, 4), np.zeros((8, 16, 1, 4), BF)], axis=2)
    return np.ascontiguousarray(np.stack([v[g][:, e[g]] for g in range(8)])).reshape(128, -1)
def tile(rs):
    return np.stack(rs, axis=2).reshape(128, -1).astype(BF)
def cut(t, i, w=512):
    return t[:, w * i:w * i + w]
def pick(q, e):
    c = np.concatenate([q[0].reshape(128, -1, 4), np.zeros((128, 1, 4), np.uint8)], axis=1); s = np.concatenate([q[1], np.ones((16, 1), np.uint8)], axis=1)
    return (np.ascontiguousarray(c[:, e].reshape(128, -1)), np.ascontiguousarray(s[:, e]))
def join(*qs):
    return (np.concatenate([q[0] for q in qs], axis=1), np.concatenate([q[1] for q in qs], axis=1))
def put(q, e, v):
    c, s = q[0].reshape(128, -1, 4).copy(), q[1].copy(); c[:, e] = v[0].reshape(128, -1, 4); s[:, e] = v[1]
    return (c.reshape(128, -1), s)
def pk(c, s):
    return (np.ascontiguousarray(c), mx_ref.live(s))
def emit(q):
    return q[0], q[1]
def packed(v, rng):
    q = [mx_ref.quantize(np.ascontiguousarray(v[r])) for r in range(N)]
    return np.stack([a for a, b in q]), np.stack([mx_ref.plane(b, rng) for a, b in q])
def values_of_codes():
    e, c = np.zeros((128, 128, 4), np.float32), np.zeros((128, 2, 4), np.uint8)
    e[np.arange(128), np.arange(128), 0] = 1
    c[:127, :, 0] = np.arange(256).reshape(2, 128).T[:127]
    return mx_ref.matmul(mx_ref.quantize(e.reshape(128, 512).astype(BF)), (c.reshape(128, 8), np.full((16, 2), 127, np.uint8))).T.reshape(-1).astype(np.float64)
CODE_VALUE, SCALE_VALUE = values_of_codes(), 2.0 ** (np.arange(256) - 127.0)
def decode(q):
    return (CODE_VALUE[q[0]].reshape(16, 8, -1, 4) * SCALE_VALUE[q[1]][:, None, :, None] + 0.0).reshape(128, -1).astype(np.float32)
def f(rng, *shape):
    return mx_ref.flush((rng.standard_normal(shape, dtype=np.float32) * np.exp2(rng.integers(-2, 3, shape[:-1] + (1,)))).astype(BF))
def wide(rng, *shape, cols=0):
    v = rng.standard_normal(shape, dtype=np.float32) * np.exp2(rng.integers(-12, 13, shape)).astype(np.float32)
    if cols: v *= np.repeat(np.exp2(rng.integers(-cols, cols + 1, shape[:-2] + (1, shape[-1] // 4))) * (rng.random(shape[:-2] + (1, shape[-1] // 4)) > 0.0625), 4, axis=-1).astype(np.float32)
    return mx_ref.flush(v.astype(BF))
C, K, R = 192, 224, 3
def big(v, k):
    v = v.astype(np.float32) * np.float32(k)
    v[np.abs(v) < np.float32(2.0 ** -16)] = 0
    return v.astype(BF)
def numbers_of(rng):
    return {"x": big(f(rng, N, 128, 4 * C), 1), "u": np.array(f(rng, N, 128, 512)), "v": np.array(f(rng, N, 128, 512))}
def ends(a, b):
    return {"ea": np.stack([gtable(e) for e in a]), "eb": np.stack([gtable(e) for e in b])}
def weights(rng, w):
    c, p = packed(w, rng)
    return {"wc": c, "ws": p}
def still(rng):
    w = np.zeros((N, 128, 4, 128, 4), np.float32)
    i = np.arange(128)
    for b in range(4): w[:, i, b, i, b] = 32
    return weights(rng, w.reshape(N, 128, 2048).astype(BF))
def signs(rng):
    return np.stack([rng.permutation(8) % 2 * 2.0 - 1.0 for r in range(N)])
def setup_inputs(rng):
    d = numbers_of(rng)
    a, b = rng.integers(0, C, (2, N, 8, 2 * K))
    return {**d, **ends(a, b), **weights(rng, f(rng, N, 128, 2048))}
def setup_inputs_ties(rng):
    d = numbers_of(rng)
    x = d["x"].reshape(N, 8, 16, C, 4)
    a, b = np.zeros((2, N, 8, 2 * K), int)
    o = rng.permutation(N)
    for r in range(N):
        k = rng.permutation(C) % 3
        three = x[r][:, :8, :3].copy()
        three[:, :, 2] = 0
        x[r][:, :8] = three[:, :, np.zeros(C, int) if r == o[0] else k]
        e = np.argsort(k, kind="stable")
        at = np.searchsorted(k[e], np.arange(3))
        q = np.stack([rng.permutation(2 * K) % 9 for g in range(8)])
        a[r] = e[at[q // 3] + rng.integers(0, C // 3, q.shape)]
        b[r] = e[at[q % 3] + rng.integers(0, C // 3, q.shape)]
    x[o[1], :, :8] = 0
    u = d["u"].reshape(N, 8, 16, 128, 4)
    u[:, :, 8:, ::16] = 0
    w = np.array(f(rng, N, 128, 2048)).reshape(N, 8, 16, 4, 8, 16, 4)
    w[:, :, 8:, :, :, :8] = 0
    return {"x": x.reshape(N, 128, 4 * C), "u": u.reshape(N, 128, 512), "v": d["v"], **ends(a, b), **weights(rng, w.reshape(N, 128, 2048))}
def setup_inputs_near(rng):
    d = numbers_of(rng)
    x = d["x"].astype(np.float32).reshape(N, 8, 16, C, 4)
    x[:, :, :2] = 0
    x[:, :, 8:10] = 0
    x[:, :, 10:] = rng.integers(4, 8, (N, 8, 6, C, 4)) * rng.choice([-1.0, 1.0], (N, 8, 6, C, 4)) * 2.0 ** -20
    u = d["u"].reshape(N, 128, 128, 4)
    u[:, :, ::16] = 0
    a, b = np.zeros((2, N, 8, 2 * K), int)
    s = np.arange(2 * K) * (C // 2) // (2 * K)
    v = ((np.arange(C // 2)[:, None] >> np.arange(8)) & 1) * np.exp2(np.arange(8) - 23.0)
    sg = signs(rng)
    for r in range(N):
        k = rng.permutation(8) % 4
        up, far = k % 2, k // 2
        for g in range(8):
            e = rng.permutation(C)
            p, z = e[:C // 2], e[C // 2:]
            x[r, g, 0, p, 0] = 1
            x[r, g, 1, p, 0] = 2.0 ** -9
            x[r, g, 8, p] = v[:, :4]
            x[r, g, 9, p] = v[:, 4:]
            if far[g]: x[r, g, 0, p[C // 2 - 1], 0] = 2.0 ** 30
            h = 16 * g
            u[r, h:h + 2, h, 0] = sg[r, g]
            u[r, h + 8:h + 10, h] = sg[r, g]
            m = p[s if up[g] else s[rng.permutation(2 * K)]]
            q = z[rng.integers(0, C // 2, 2 * K)]
            first = rng.random(2 * K) < 0.5
            a[r, g] = np.where(first, m, q)
            b[r, g] = np.where(first, q, m)
    return {"x": x.reshape(N, 128, 4 * C).astype(BF), "u": u.reshape(N, 128, 512), "v": d["v"], **ends(a, b), **still(rng)}
def setup_inputs_huge(rng):
    d = numbers_of(rng)
    far = (rng.permutation(N) < N // 2)[:, None, None, None]
    c = np.stack([rng.permutation(C) % 2 * 2.0 - 1.0 for r in range(N)])
    x = np.where(far, 2.0 ** 30, 2.0 ** -15) * (0.6 + 0.4 * rng.random((N, 128, C, 4))) * c[:, None, :, None]
    u = d["u"].reshape(N, 128, 128, 4)
    s = np.where(far, 2.0 ** 30, 2.0 ** -29) * (1 - 0.25 * rng.random((N, 128, 8, 4))) * signs(rng)[:, None, :, None]
    two = np.isin(np.arange(128)[:, None] - 16 * np.arange(8), (0, 1))[None, :, :, None]
    s = np.where(far | two, s, 0.0)
    u[:, :, ::16] = s.astype(np.float32).astype(BF)
    a, b = np.zeros((2, N, 8, 2 * K), int)
    for r in range(N):
        p = np.flatnonzero(c[r] > 0)[rng.integers(0, C // 2, (8, 2 * K))]
        q = np.flatnonzero(c[r] < 0)[rng.integers(0, C // 2, (8, 2 * K))]
        first = rng.random((8, 2 * K)) < 0.5
        a[r] = np.where(first, p, q)
        b[r] = np.where(first, q, p)
    return {"x": x.astype(np.float32).reshape(N, 128, 4 * C).astype(BF), "u": u.reshape(N, 128, 512), "v": d["v"], **ends(a, b), **still(rng)}
def setup_inputs_knots(rng):
    d = numbers_of(rng)
    x = d["x"].reshape(N, 128, C, 4)
    x[:, :, 0] = 0
    x[:, :, 1] = np.abs(x[:, :, 1].astype(np.float32)).astype(BF)
    u = d["u"].reshape(N, 128, 128, 4)
    u[:, :, ::16] = np.abs(u[:, :, ::16].astype(np.float32)).astype(BF)
    a, b = rng.integers(0, C, (2, N, 8, 2 * K))
    for r in range(N):
        g = rng.permutation(8)
        a[r, g[0]] = 0
        b[r, g[0]] = 1
        b[r, g[1]] = a[r, g[1]]
        for h, lo in ((g[2], 0), (g[3], K)):
            a[r, h] = 0
            b[r, h] = 1
            b[r, h, lo:lo + K] = 0
        a[r, g[4]] = C - 1
        a[r, g[5]] = np.arange(2 * K) % C
        b[r, g[5]] = (np.arange(2 * K) + 1) % C
    return {"x": x.reshape(N, 128, 4 * C), "u": u.reshape(N, 128, 512), "v": d["v"], **ends(a, b), **weights(rng, f(rng, N, 128, 2048))}
def setup_inputs_spread(rng):
    d = setup_inputs(rng)
    d["x"] = big(wide(rng, N, 128, 4 * C, cols=6), 1)
    return d
def check_inputs(d):
    b = []
    for k in ("x", "u", "v"):
        a = np.abs(d[k].astype(np.float32))
        if not (np.isfinite(a).all() and ((a == 0) | (a >= 2.0 ** -30) & (a <= 2.0 ** 30)).all()): b.append("a value of " + k)
    for k in ("ea", "eb"):
        if not ((d[k] >= 0) & (d[k] < C)).all(): b.append("an entry of " + k)
    a = np.abs(np.stack([decode(pk(d["wc"][r], d["ws"][r])) for r in range(N)]))
    if not ((a == 0) | (a >= 2.0 ** -30) & (a <= 2.0 ** 30)).all(): b.append("a number that wc and ws hold")
    return b
def reference(x, u, v, ea, eb, wc, ws):
    qu = [mx_ref.quantize(u[r]) for r in range(N)]
    lay = [pk(wc[r], ws[r]) for r in range(N)]
    a, b = [gentries(ea[r]) for r in range(N)], [gentries(eb[r]) for r in range(N)]
    new = [mx_ref.quantize(x[r]) for r in range(N)]
    held = [q for q in new]
    nums = [np.zeros((128, 0), BF) for r in range(N)]
    s = [np.zeros((8, 0), np.float32) for r in range(N)]
    for t in range(1, R + 1):
        got = decode(join(*new)).astype(BF)
        n = C + (t - 1) * K
        for r in range(N):
            nums[r] = np.concatenate([nums[r], cut(got, r, 4 * C if t == 1 else 4 * K)], axis=1)
            s[r] = np.concatenate([s[r], mx_ref.matmul(qu[r], new[r])[::16]], axis=1)
        for r in range(N):
            z = np.abs(np.take_along_axis(s[r], a[r], axis=1) - np.take_along_axis(s[r], b[r], axis=1))
            e = np.sort(np.argsort(-z, axis=1, kind="stable")[:, :K], axis=1)
            p, q = np.take_along_axis(a[r], e, axis=1), np.take_along_axis(b[r], e, axis=1)
            mid = (gcols(nums[r], p).astype(np.float32) + gcols(nums[r], q).astype(np.float32)) * np.float32(0.5)
            m = mx_ref.quantize(np.ascontiguousarray(mid.astype(BF)))
            w = lay[(r + t) % N]
            new[r] = mx_ref.quantize(tile([mx_ref.matmul(pick(w, np.arange(128 * i, 128 * i + 128)), m) * np.float32(0.03125) for i in range(4)]))
            held[r] = join(held[r], new[r])
            at = np.tile(n + np.arange(K), (8, 1))
            a[r], b[r] = np.stack([p, at], axis=2).reshape(8, -1), np.stack([at, q], axis=2).reshape(8, -1)
    y, el = np.zeros((N, 128, C + R * K), np.float32), np.zeros((N, 8, 4 * K), np.float32)
    oc, osc = np.zeros((N, 128, 4 * (C + R * K)), np.uint8), np.zeros((N, 16, C + R * K), np.uint8)
    for r in range(N):
        y[r] = mx_ref.matmul(mx_ref.quantize(v[r]), held[r])
        el[r] = np.concatenate([a[r], b[r]], axis=1)
        oc[r], osc[r] = emit(held[r])
    return {"y": y, "el": el, "oc": oc, "osc": osc}

@@ -1,0 +1,641 @@
+from concourse.bass import DstId, RemoteDMATransfer
+from concourse.mybir import dt, AluOpType as ALU, AxisListType as AX, ActivationFunctionType as AF
+
+C, K, R, N = 192, 224, 3, 8
+E = 2 * K
+Q4, U8, BF, F32, I32, U16 = "float8_e4m3fn_x4", "uint8", "bfloat16", "float32", "int32", "uint16"
+CW = 1136
+
+SCRATCH = {}
+for _n, _c, _d in [
+    ("xt", 4 * C, BF), ("ut", 512, BF), ("vt", 512, BF), ("eai", 28, I32), ("ebi", 28, I32),
+    ("wq", 512, Q4), ("wsc", 512, U8),
+    ("lq1", 512, Q4), ("ls1", 512, U8), ("lq2", 512, Q4), ("ls2", 512, U8), ("lq3", 512, Q4), ("ls3", 512, U8),
+    ("rq0", 256, Q4), ("rs0", 256, U8), ("rq1", 256, Q4), ("rs1", 256, U8),
+    ("uq", 128, Q4), ("us", 128, U8), ("uq2", 128, Q4), ("us2", 128, U8), ("vq", 128, Q4), ("vs", 128, U8),
+    ("tq0", C, Q4), ("ts0", C, U8), ("tq1", K, Q4), ("ts1", K, U8), ("tq2", K, Q4), ("ts2", K, U8),
+    ("tq3", K, Q4), ("ts3", K, U8),
+    ("mq1", K, Q4), ("ms1", K, U8), ("mq2", K, Q4), ("ms2", K, U8), ("mq3", K, Q4), ("ms3", K, U8),
+    ("mt1", 4 * K, BF), ("mt2", 4 * K, BF), ("mt3", 4 * K, BF),
+    ("ft1", 4 * K, BF), ("ft2", 4 * K, BF), ("ft3", 4 * K, BF),
+    ("ez", 516, BF), ("eq", 512, Q4), ("es", 512, U8),
+    ("d1", 4 * C, BF), ("w2", 4 * 3 * K, BF), ("w3", 4 * 2 * K, BF), ("mid2", 4 * E, BF), ("mid3", 4 * E, BF),
+    ("p1", C, F32), ("pw2", 3 * K, F32), ("pw3", 2 * K, F32), ("nw2", 3 * K, F32), ("nw3", 3 * K, F32),
+    ("elb", 2 * E, F32), ("ysb", C + R * K, F32),
+    ("pa1", E, F32), ("dz", E, F32), ("z", E, F32), ("dd", E, F32), ("zm", E, F32), ("zs", E, F32),
+    ("junk", E, BF), ("arep", E, F32), ("pk", E, F32), ("src1", E, F32), ("src2", E, BF),
+    ("cwf", CW, F32), ("cwb", CW, BF), ("uf", E, F32), ("ub", E, BF),
+    ("ramp", 516, F32), ("rampb", C, F32), ("jm", E, BF), ("mask", E, BF), ("nmask", E, BF), ("wn", 1024, F32),
+    ("ci", 16, I32), ("uli", 8, I32), ("cf", 32, F32), ("cst", 64, F32), ("pows", 48, F32), ("t16", 48, F32),
+    ("c2", 64, F32), ("cx", 56, F32), ("win2", 64, F32), ("xw", 56, F32), ("sv", 32, F32), ("g16", 32, F32),
+    ("j16", 16, F32), ("j32", 48, F32), ("rst", 56, F32), ("jc", 28, F32), ("sg2f", 28, F32),
+    ("down", 56, F32), ("cmp", 56, F32), ("cum", 56, F32), ("sm", 8 * 28, F32),
+    ("ai", 16, I32), ("bfr", 16, F32),
+    ("ul", 8, U16), ("ea16", 28, U16), ("eb16", 28, U16), ("sg1", 28, U16), ("sg2", 28, U16), ("xl", 2, U16),
+    ("off", 2, U16), ("tot", 2, U16), ("tot0", 2, U16), ("dest", 28, U16),
+    ("la", 16, U16), ("lb", 16, U16), ("ix2", 16, U16), ("ix3", 16, U16),
+]:
+    SCRATCH[_n] = ("sbuf", [128, _c], _d)
+BANKS = ("r0", "r1", "r2", "r3", "pp", "py")
+for _n in BANKS:
+    SCRATCH[_n] = ("psum", [128, 512], F32)
+
+SEMAPHORES = ["sV", "sA", "sP", "sG", "ld_x", "ld_u", "ld_e", "ld_w", "ld_v", "st",
+              "arr1", "arr2", "arr3", "rin0", "rin1", "sent"]
+
+
+def bits(engs):
+    m = 0
+    for e in engs:
+        m |= 1 << e
+    return m
+
+
+def helpers(T, topo, src, dst):
+    by_die = {}
+    for c in topo.cores_of(src):
+        if T.rank_of(c) is None and topo.may_write(c, dst) and topo.die(c) not in by_die:
+            by_die[topo.die(c)] = c
+    return [by_die[d] for d in sorted(by_die)]
+
+
+def routes(T, topo):
+    out, slot = [], {}
+    for s in range(N):
+        src = T.cores[s]
+        slot[s] = [c for c in topo.cores_of(src) if T.rank_of(c) is not None].index(src)
+        for t in range(1, R + 1):
+            d = (s - t) % N
+            dst = T.cores[d]
+            out.append((s, t, d, None if topo.may_write(src, dst) else helpers(T, topo, src, dst)))
+    return out, slot
+
+
+def send_pair(g, T, topo, src, dst, oq, os_, iq, is_, sem):
+    rid, pid = topo.addr(dst, src)
+    m = topo.mask(src, dst)
+    g.remote_dma(oq.bitcast(dt.uint8), iq.bitcast(dt.uint8), sem, T.sem.sent, pid, rid, m)
+    g.remote_dma(os_, is_, sem, T.sem.sent, pid, rid, m)
+    return 2 * len(topo.engines(src, dst))
+
+
+def helper_program(g, core, T, topo):
+    rts, slot = routes(T, topo)
+    jobs = sorted((t, s, d, h.index(core)) for s, t, d, h in rts if h and core in h)
+    if not jobs:
+        return
+    waited, sent = set(), 0
+    for t, s, d, half in jobs:
+        k = slot[s]
+        if k not in waited:
+            waited.add(k)
+            g.wait_ge(T.sem["rin%d" % k], len(topo.engines(T.cores[s], core)))
+        a = 256 * half
+        sent += send_pair(g, T, topo, core, T.cores[d], T["lq%d" % t][:, a:a + 256], T["ls%d" % t][:, a:a + 256],
+                          T["rq%d" % k][:], T["rs%d" % k][:], T.sem["arr%d" % t])
+        if t == 1:
+            g.wait_ge(T.sem.sent, sent)
+    g.wait_ge(T.sem.sent, sent)
+
+
+def rank_program(g, core, T, topo):
+    rank = T.rank_of(core)
+    if rank is None:
+        helper_program(g, core, T, topo)
+        return
+    rts, slot = routes(T, topo)
+    qs = {"V": g.vector, "A": g.scalar, "P": g.tensor, "G": g, "S": g.sync}
+    cnt = {"V": 0, "A": 0, "P": 0, "G": 0}
+    known = {q: {} for q in qs}
+    snap, lastw, readers = {}, {}, {}
+    stores = [0]
+
+    def need(q, evs):
+        kn = known[q]
+        best = {}
+        for s, v in evs:
+            if v > best.get(s, 0):
+                best[s] = v
+        for s, v in sorted(best.items(), key=lambda sv: -len(snap.get(sv, {}))):
+            if kn.get(s, 0) >= v:
+                continue
+            qs[q].wait_ge(T.sem[s], v)
+            kn[s] = v
+            for s2, v2 in snap.get((s, v), {}).items():
+                if v2 > kn.get(s2, 0):
+                    kn[s2] = v2
+
+    def deps(rd, wr):
+        evs = [lastw[k] for k in rd]
+        for k in wr:
+            if k in lastw:
+                evs.append(lastw[k])
+            evs.extend(readers.get(k, []))
+        return evs
+
+    def op(q, fn, rd, wr):
+        wr = list(wr) + [k for k in rd if k in BANKS]
+        need(q, deps(rd, wr))
+        cnt[q] += 1
+        ev = ("s" + q, cnt[q])
+        fn().then_inc(T.sem["s" + q], 1)
+        snap[ev] = dict(known[q])
+        for k in rd:
+            readers.setdefault(k, []).append(ev)
+        for k in wr:
+            lastw[k] = ev
+            readers[k] = []
+
+    def load(q, out, in_, sem, key, total):
+        qs[q].dma_start(out, in_).then_inc(T.sem[sem], 16)
+        lastw[key] = (sem, total)
+
+    def store(q, out, in_, rd):
+        need(q, deps(rd, []))
+        qs[q].dma_start(out, in_).then_inc(T.sem.st, 16)
+        stores[0] += 16
+
+    V, A, P = g.vector, g.scalar, g.tensor
+    ID = AF.Identity
+
+    def ts(out, in0, s1, s2, o0, o1, rd, wr):
+        if o1 is None:
+            op("V", lambda: V.tensor_scalar(out, in0, s1, None, o0), rd, wr)
+        else:
+            op("V", lambda: V.tensor_scalar(out, in0, s1, s2, o0, o1), rd, wr)
+
+    def tt(out, in0, in1, o, rd, wr):
+        op("V", lambda: V.tensor_tensor(out, in0, in1, o), rd, wr)
+
+    def cp(out, in_, rd, wr):
+        op("V", lambda: V.tensor_copy(out, in_), rd, wr)
+
+    def ms(out, c, wr):
+        op("V", lambda: V.memset(out, c), [], wr)
+
+    def red(out, in_, o, rd, wr, negate=False):
+        op("V", lambda: V.tensor_reduce(out, in_, AX.X, o, negate=negate), rd, wr)
+
+    def scan(out, d0, d1_, init, o0, rd, wr):
+        op("V", lambda: V.tensor_tensor_scan(out, d0, d1_, init, o0, ALU.add), rd, wr)
+
+    def act(out, in_, func, rd, wr, **kw):
+        op("A", lambda: A.activation(out, in_, func, **kw), rd, wr)
+
+    def mv(q, out, in_, rd, wr):
+        if q == "V":
+            cp(out, in_, rd, wr)
+        else:
+            act(out, in_, AF.Copy, rd, wr)
+
+    def gat(q, out, win, lst, rd, wr):
+        return lambda: mv(q, out, win.indirect(lst), rd, wr)
+
+    def quant(oq, os_, in_, rd, wr):
+        op("V", lambda: V.quantize_mx(oq, os_, in_), rd, wr)
+
+    def mm(bank, n, lq, ls, rq, rs, rd):
+        op("P", lambda: P.matmul_mx(T[bank][:, 0:n], lq, ls, rq, rs, True, True), rd, [bank])
+
+    def iota(out, pat, base, cm, wr, flt=True):
+        if flt:
+            op("G", lambda: g.iota(out, pat, base, cm, allow_small_or_imprecise_dtypes=True), [], wr)
+        else:
+            op("G", lambda: g.iota(out, pat, base, cm), [], wr)
+
+    def col(name, j):
+        return T[name][:, j:j + 1]
+
+    load("A", T.ut[:], T.u[:], "ld_u", "ut", 16)
+    load("S", T.xt[:], T.x[:], "ld_x", "xt", 16)
+    load("A", T.eai[:], T.ea[:], "ld_e", "eai", 32)
+    load("A", T.ebi[:], T.eb[:], "ld_e", "ebi", 32)
+    load("S", T.wq[:].bitcast(dt.uint8), T.wc[:], "ld_w", "wq", 32)
+    load("S", T.wsc[:], T.ws[:], "ld_w", "wsc", 32)
+    load("S", T.vt[:], T.v[:], "ld_v", "vt", 16)
+
+    iota(col("ci", 0), [[1, 1]], 0, 1, ["pi"], False)
+    iota(T.uli[:], [[16, 8]], 0, 0, ["uli"], False)
+    iota(T.ramp[:], [[1, 516]], 0, 0, ["ramp"])
+    iota(T.jm[:], [[0, 28], [1, 16]], 0, 0, ["jm"])
+    (cR, cPAR, cP4, cNP1, cSC2, cR2, cC0, cF, cCP, cR28, cR14, cJ, cX1, cX2, cR32, cN32, cR64, cCR, cAR, cK1, cK2,
+     cT1, cT2) = [col("cf", j) for j in range(23)]
+    RR = T.cf[:, 24:26]
+    ts(col("ci", 1), col("ci", 0), 15, None, ALU.bitwise_and, None, ["pi"], ["ri"])
+    ts(col("ci", 2), col("ci", 0), 16, None, ALU.bitwise_and, None, ["pi"], ["pari"])
+    ts(cP4, col("ci", 0), 4.0, 3.0, ALU.mult, ALU.add, ["pi"], ["p4"])
+    ms(T.cst[:, 0:16], 2.0 ** 14, ["k14"])
+    ms(T.cst[:, 16:32], 2.0, ["k2"])
+    ms(T.cst[:, 32:48], 0.5, ["kh"])
+    ms(T.cst[:, 48:64], 0.0, ["k0"])
+    cp(cR, col("ci", 1), ["ri"], ["r"])
+    cp(cPAR, col("ci", 2), ["pari"], ["par"])
+    cp(T.ul[:], T.uli[:], ["uli"], ["ul"])
+    zero = T.cst[:, 48:64]
+    for j, (key, init) in enumerate((("k14", 2.0 ** -114), ("k2", 0.5), ("kh", 2.0))):
+        scan(T.pows[:, 16 * j:16 * j + 16], T.cst[:, 16 * j:16 * j + 16], zero, init, ALU.mult,
+             [key, "k0"], ["pow%d" % j])
+    ms(T.c2[:], 0.0, ["c2"])
+    ms(T.cx[:], 0.0, ["cx"])
+    ts(RR, zero[:, 0:2], cR, None, ALU.add, None, ["k0", "r"], ["rr"])
+    ts(cC0, cR, 0.0, 2.0, ALU.is_equal, ALU.mult, ["r"], ["c0"])
+    ts(cR28, cR, 28.0, None, ALU.mult, None, ["r"], ["r28"])
+    ts(T.t16[:, 0:16], T.ramp[:, 0:16], cR, None, ALU.is_equal, None, ["ramp", "r"], ["m16"])
+    ts(T.sg1[:], T.ramp[:, 0:28], cR28, None, ALU.add, None, ["ramp", "r28"], ["sg1"])
+    tt(T.t16[:, 16:32], T.t16[:, 0:16], T.pows[:, 0:16], ALU.mult, ["m16", "pow0"], ["t16a"])
+    tt(T.t16[:, 32:48], T.t16[:, 0:16], T.pows[:, 32:48], ALU.mult, ["m16", "pow2"], ["t16b"])
+    ts(T.ez[:], T.ramp[:], cP4, 0.5, ALU.is_equal, ALU.mult, ["ramp", "p4"], ["ez"])
+    red(cNP1, T.t16[:, 16:32], ALU.add, ["t16a"], ["np1"], True)
+    red(cSC2, T.t16[:, 32:48], ALU.add, ["t16b"], ["sc2"], True)
+    act(cF, cR, ID, ["r"], ["f"], scale=1.0 / 16, bias=1.0)
+    act(cR2, cR, ID, ["r"], ["r2c"], scale=2.0)
+    step = [2.0 ** -4, 2.0 ** -8, 2.0 ** -12, 2.0 ** -16, 2.0 ** -20, 2.0 ** -23]
+    cxk = []
+    for j in range(6):
+        act(col("cx", 8 * j + 1), cR, ID, ["r", "cx"], ["cxa%d" % j], scale=0.0, bias=step[j])
+        if j < 4:
+            sc, bi = step[j + 1] - step[j], 0.0
+        elif j == 4:
+            sc, bi = 0.0, -1.5
+        else:
+            sc, bi = -step[5], step[5]
+        act(T.cx[:, 8 * j + 2:8 * j + 4], RR, ID, ["rr", "cx"], ["cxb%d" % j], scale=sc, bias=bi)
+        cxk += ["cxa%d" % j, "cxb%d" % j]
+    act(col("cx", 36), cR, ID, ["r", "cx"], ["cxc"], scale=step[5] - step[4], bias=-step[5] / 2)
+    act(col("cx", 48), cR, ID, ["r", "cx"], ["cxd"], scale=0.0, bias=-1.5)
+    cxk += ["cx", "cxc", "cxd"]
+    act(T.c2[:, 0:2], RR, ID, ["rr", "c2"], ["c2a"], scale=1.0 / 16, bias=1.0)
+    act(T.c2[:, 32:34], RR, ID, ["rr", "c2"], ["c2b"], scale=0.0, bias=1.0)
+    act(T.c2[:, 3:32:2], T.pows[:, 16:31], ID, ["pow1", "c2", "f"], ["c2c"], scale=cF)
+    act(T.c2[:, 35:64:2], T.pows[:, 16:31], ID, ["pow1", "c2"], ["c2d"])
+    c2k = ["c2", "c2a", "c2b", "c2c", "c2d"]
+    act(cR32, cR, ID, ["r"], ["r32"], scale=32.0)
+    act(cN32, cR, ID, ["r"], ["n32"], scale=-32.0)
+    act(cR64, cR, ID, ["r"], ["r64"], scale=64.0)
+
+    need("G", [("ld_w", 32)])
+    sent = [0]
+    late = []
+    fed = False
+    for t, d, h in sorted((t, d, h) for s, t, d, h in rts if s == rank):
+        dst = T.cores[d]
+        if h is None:
+            if t == 1:
+                sent[0] += send_pair(g, T, topo, core, dst, T["lq%d" % t][:], T["ls%d" % t][:], T.wq[:], T.wsc[:],
+                                     T.sem["arr%d" % t])
+            else:
+                late.append((t, dst))
+        elif not fed:
+            fed = True
+            k = slot[rank]
+            for name, srcn, cast in (("rq%d" % k, "wq", True), ("rs%d" % k, "wsc", False)):
+                trs = []
+                for half, hc in enumerate(h):
+                    eng = topo.engines(core, hc)
+                    eng = eng[half * len(eng) // 2:(half + 1) * len(eng) // 2]
+                    rid, pid = topo.addr(hc, core)
+                    s_ap, d_ap = T[srcn][:, 256 * half:256 * half + 256], T[name][:]
+                    if cast:
+                        s_ap, d_ap = s_ap.bitcast(dt.uint8), d_ap.bitcast(dt.uint8)
+                    trs.append(RemoteDMATransfer(dst_ids=[DstId(rid=rid, pnc=pid)], dma_engine_mask=bits(eng),
+                                                 remote_sem=T.sem["rin%d" % k], src=s_ap, dst=d_ap))
+                    sent[0] += len(eng)
+                g.remote_dma_fused(trs, local_sem=T.sem.sent)
+    for s, t, d, h in rts:
+        if d == rank:
+            lastw["l%d" % t] = ("arr%d" % t, sum(2 * len(topo.engines(c, core)) for c in (h or [T.cores[s]])))
+    iota(T.wn[:, 0:512], [[-32, 16], [1, 32]], -29, 0, ["wn0", "wn1"])
+    iota(T.wn[:, 512:1024], [[1, 512]], 0, 0, ["wn2"])
+    iota(T.sg2f[:], [[1, 14], [K, 2]], 0, 0, ["sg2f"])
+    iota(T.nw2[:, K:2 * K], [[1, K]], C, 0, ["nw2H"])
+    iota(T.src2[:], [[1, 14], [K, 2], [14, 16]], -K, 0, ["src2"])
+    iota(T.nw3[:, K:2 * K], [[1, K]], C + K, 0, ["nw3H"])
+    iota(T.elb[:, 1:E:2], [[1, K]], C + 2 * K, 0, ["el1"])
+    iota(T.elb[:, E:2 * E:2], [[1, K]], C + 2 * K, 0, ["el2"])
+    for t, dst in late:
+        need("G", [lastw["l%d" % (t - 1)]])
+        sent[0] += send_pair(g, T, topo, core, dst, T["lq%d" % t][:], T["ls%d" % t][:], T.wq[:], T.wsc[:],
+                             T.sem["arr%d" % t])
+
+    def span(t):
+        return (0, C) if t == 0 else (C + (t - 1) * K, K)
+
+    def put_table(t, qa, qb):
+        a, n = span(t)
+        key = ["t%d" % t]
+        store(qa, T.oc[:, 4 * a:4 * (a + n)], T["tq%d" % t][:].bitcast(dt.uint8), key)
+        for k in range(4):
+            store(qb if k % 2 else qa, T.osc[4 * k:4 * k + 4, a:a + n], T["ts%d" % t][32 * k:32 * k + 4, :], key)
+
+    def y_mm(t):
+        mm("py", span(t)[1], T.vq[:], T.vs[:], T["tq%d" % t][:], T["ts%d" % t][:], ["vq", "t%d" % t])
+
+    def y_out(t, q, sq):
+        a, n = span(t)
+        mv(q, T.ysb[:, a:a + n], T.py[:, 0:n], ["py"], ["y%d" % t])
+        store(sq, T.y[:, a:a + n], T.ysb[:, a:a + n], ["y%d" % t])
+
+    def unpack(t):
+        for b in range(4):
+            mm("r%d" % b, span(t)[1], T.eq[:, 128 * b:128 * b + 128], T.es[:, 128 * b:128 * b + 128],
+               T["tq%d" % t][:], T["ts%d" % t][:], ["eq%d" % b, "t%d" % t])
+
+    def p_mm(t):
+        mm("pp", span(t)[1], T.uq2[:], T.us2[:], T["tq%d" % t][:], T["ts%d" % t][:], ["uq2", "us2", "t%d" % t])
+
+    TINY, UP = 2.0 ** -100, 2.0 ** 30
+
+    def absz(h):
+        act(T.z[:, K * h:K * h + K], T.dz[:, K * h:K * h + K], AF.Abs, ["dz%d0" % h, "dz%d1" % h], ["z%d" % h],
+            scale=UP, bias=TINY)
+
+    quant(T.uq[:], T.us[:], T.ut[:], ["ut"], ["uq"])
+    cp(T.uq2[:].bitcast(dt.uint32), T.uq[:].bitcast(dt.uint32).indirect(T.ul[:]), ["uq", "ul"], ["uq2"])
+    act(T.us2[:], T.us[:].indirect(T.ul[:]), AF.Copy, ["uq", "ul"], ["us2"])
+    quant(T.tq0[:], T.ts0[:], T.xt[:], ["xt"], ["t0"])
+    cp(T.ea16[:], T.eai[:], ["eai"], ["ea16"])
+    cp(T.eb16[:], T.ebi[:], ["ebi"], ["eb16"])
+    p_mm(0)
+    put_table(0, "S", "S")
+    gat("A", T.arep[:, 0:K], T.ramp[:, 0:C], T.ea16[:, 0:14], ["ramp", "ea16"], ["arep0"])()
+    cp(T.p1[:], T.pp[:, 0:C], ["pp"], ["p1"])
+    ts(T.mask[:], T.jm[:], cR, None, ALU.is_equal, None, ["jm", "r"], ["mask"])
+    cuts = ((0, 6), (6, 14), (14, 22), (22, 28))
+    for i, (a, b) in enumerate(cuts):
+        act(T.pa1[:, 16 * a:16 * b], T.p1[:].indirect(T.ea16[:, a:b]), AF.Copy, ["p1", "ea16"], ["pa1%d" % i])
+    for i, (a, b) in enumerate(cuts):
+        tt(T.dz[:, 16 * a:16 * b], T.p1[:].indirect(T.eb16[:, a:b]), T.pa1[:, 16 * a:16 * b],
+           ALU.subtract, ["p1", "eb16", "pa1%d" % i], ["dz%d%d" % (i // 2, i % 2)])
+    absz(0)
+    absz(1)
+    ts(T.nmask[:], T.jm[:], cR, None, ALU.not_equal, None, ["jm", "r"], ["nmask"])
+    Z = ["z0", "z1"]
+    sS, sL, sLO, sGN, sAL = [col("sv", j) for j in range(5)]
+    piv = lambda j: col("sv", 8 + j)
+    WN = ["wn0", "wn1", "wn2", "n32"]
+
+    def choose(t, vs, as_):
+        sg, sgk = (T.sg1, "sg1") if t == 1 else (T.sg2, "sg2")
+
+        def count(j, src, rd, **kw):
+            act(T.junk[:], src, AF.Sign, rd, ["junk", "S"], accum_out=sS, **kw)
+            for f in as_.get(j, []):
+                f()
+
+        def run(j):
+            for f in vs.get(j, []):
+                f()
+
+        def own(h):
+            tt(T.zm[:, K * h:K * h + K], T.z[:].indirect(sg[:, 14 * h:14 * h + 14]), T.mask[:, K * h:K * h + K],
+               ALU.mult, Z + [sgk, "mask"], ["zm%d" % h])
+
+        o1 = T.off[:, 0:1]
+        count(1, T.z[:], Z + ["np1"], bias=cNP1)
+        own(0)
+        run(1)
+        ts(o1, sS, 0.0, cR, ALU.is_ge, ALU.mult, ["S", "r"], ["off"])
+        cp(T.g16[:, 0:16], T.pows[:, 0:16].indirect(o1), ["pow0", "off"], ["g16a"])
+        red(sL, T.g16[:, 0:16], ALU.max, ["g16a"], ["L"])
+        count(2, T.z[:], Z + ["sc2", "L"], scale=cSC2, bias=sL)
+        own(1)
+        ts(T.win2[:], T.c2[:], sL, None, ALU.mult, None, c2k + ["L"], ["win2"])
+        run(2)
+        ts(o1, sS, 0.0, cR2, ALU.is_le, ALU.add, ["S", "r2c"], ["off"])
+        act(T.j16[:], T.win2[:, 0:32].indirect(o1), ID, ["win2", "off"], ["j16", "piv3"], accum_out=piv(3))
+        cp(T.g16[:, 16:32], T.win2[:, 32:64].indirect(o1), ["win2", "off"], ["g16b"])
+        red(sLO, T.g16[:, 16:32], ALU.add, ["g16b"], ["lo"])
+        ts(T.xw[:], T.cx[:], sLO, None, ALU.mult, None, cxk + ["lo"], ["xw"] + ["xb%d" % j for j in range(3, 9)])
+        negc, unit = col("xw", 48), col("xw", 41)
+        for j in range(3, 9):
+            a = 8 * (j - 3)
+            pk_ = "piv%d" % j
+            count(j, T.z[:] if j < 8 else T.dd[:], (Z if j < 8 else ["dd"]) + [pk_], scale=-1.0, bias=piv(j))
+            if j == 4:
+                scan(T.zs[:], T.nmask[:], T.zm[:], 0.0, ALU.mult, ["nmask", "zm0", "zm1"], ["zs"])
+            if j == 5:
+                ts(T.dd[:], T.z[:], negc, None, ALU.add, None, Z + ["xw"], ["dd"])
+            if j == 6:
+                ts(T.down[:, 0:28], T.zs[:, 15:E:16], negc, unit, ALU.add, ALU.add, ["zs", "xw"], ["dn0"])
+                ts(T.down[:, 28:56], T.zs[:, 15:E:16], negc, None, ALU.add, None, ["zs", "xw"], ["dn1"])
+            if j > 3:
+                run(j)
+            xb = T.xw[:, a + 2:a + 4]
+            if j == 7:
+                ts(xb, xb, piv(j), col("xw", 36), ALU.add, ALU.add, ["xw", pk_], ["xb%d" % j])
+            else:
+                ts(xb, xb, piv(j), None, ALU.add, None, ["xw", pk_], ["xb%d" % j])
+            if j == 3:
+                run(j)
+            ts(o1, sS, 0.0, cC0, ALU.is_le, ALU.add, ["S", "c0"], ["off"])
+            act(T.j16[:], T.xw[:, a:a + 8].indirect(o1), ID, ["xw", "xb%d" % j, "off"], ["j16", "piv%d" % (j + 1)],
+                accum_out=piv(j + 1))
+        sm = lambda j: T.sm[:, 28 * j:28 * j + 28]
+        ge, gt = T.cmp[:, 0:28], T.cmp[:, 28:56]
+        cge, cg = T.cum[:, 0:28], T.cum[:, 28:56]
+        ts(T.cmp[:], T.down[:], piv(9), None, ALU.is_gt, None, ["dn0", "dn1", "piv9"], ["cmp"])
+        scan(T.cum[:], T.rst[:], T.cmp[:], cR32, ALU.max, ["rst", "cmp", "r32"], ["cum"])
+        tt(sm(0), ge, gt, ALU.add, ["cmp"], ["sm0"])
+        cp(T.tot[:], T.cum[:, 27:56:28], ["cum"], ["tot"])
+        act(T.j32[:, 0:32], T.wn[:].indirect(T.tot[:]), AF.Relu, WN + ["tot"], ["j32a", "gn"], bias=cN32, accum_out=sGN)
+        act(T.j32[:, 32:48], T.wn[:].indirect(T.tot[:, 0:1]), AF.Relu, WN + ["tot"], ["j32b", "al"], bias=cN32,
+            accum_out=sAL)
+        tt(sm(1), cg, cge, ALU.subtract, ["cum"], ["sm1"])
+        ts(sm(2), sm(0), 4096.0, cK2, ALU.mult, ALU.add, ["sm0", "k2c"], ["sm2"])
+        tt(sm(3), sm(1), sm(2), ALU.add, ["sm1", "sm2"], ["sm3"])
+        ts(sm(4), sm(1), cK1, sGN, ALU.add, ALU.max, ["sm1", "gn", "k1c"], ["sm4"])
+        ts(sm(5), sm(3), sGN, 2048.0, ALU.is_lt, ALU.mult, ["sm3", "gn"], ["sm5"])
+        tt(sm(6), cg, sm(4), ALU.subtract, ["sm4", "cum"], ["sm6"])
+        tt(sm(7), sm(5), T.jc[:], ALU.add, ["sm5", "jc"], ["sm7"])
+        tt(sm(0), sm(6), sm(7), ALU.max, ["sm6", "sm7"], ["sm0"])
+        ts(T.dest[:], sm(0), sAL, cCP, ALU.add, ALU.add, ["sm0", "al", "cp"], ["dest"])
+        cw, ck, ub, src = (T.cwf, "cwf", T.uf, "src1") if t == 1 else (T.cwb, "cwb", T.ub, "src2")
+        cp(cw[:].indirect(T.dest[:]), T[src][:], [src, "dest"], [ck])
+        for h in range(2):
+            op("V", lambda: V.transpose(ub[:, K * h:K * h + K], cw[:, 16 * h:16 * h + K]), [ck], ["u%d" % h])
+        return ub[:].indirect(T.xl[:, 0:1]), ["u0", "u1", "xl"]
+
+    def layer(t, mid, after):
+        quant(T["mq%d" % t][:], T["ms%d" % t][:], T["mt%d" % t][:], ["m%d" % b for b in range(4)], ["mq"])
+        for b in range(4):
+            mm("r%d" % b, K, T["lq%d" % t][:, 128 * b:128 * b + 128], T["ls%d" % t][:, 128 * b:128 * b + 128],
+               T["mq%d" % t][:], T["ms%d" % t][:], ["l%d" % t, "mq"])
+        for f in mid:
+            f()
+        ft = T["ft%d" % t]
+        for b in range(4):
+            o, i = ft[:, b:4 * K:4], T["r%d" % b][:, 0:K]
+            if b % 2 == 0:
+                act(o, i, AF.Copy, ["r%d" % b], ["f%d" % b], scale=0.03125)
+            else:
+                ts(o, i, 0.03125, None, ALU.mult, None, ["r%d" % b], ["f%d" % b])
+        quant(T["tq%d" % t][:], T["ts%d" % t][:], ft[:], ["f%d" % b for b in range(4)], ["t%d" % t])
+        for f in after:
+            f()
+
+    def scores(pa, pb, ka, kb):
+        tt(T.dz[:, 0:K], pa, T.pp[:, 0:K], ALU.subtract, [ka, "pp"], ["dz00", "dz01"])
+        tt(T.dz[:, K:E], pb, T.pp[:, 0:K], ALU.subtract, [kb, "pp"], ["dz10", "dz11"])
+        absz(0)
+        absz(1)
+
+    def eq_q(b):
+        return lambda: quant(T.eq[:, 128 * b:128 * b + 128], T.es[:, 128 * b:128 * b + 128], T.ez[:, 3 - b:515 - b],
+                             ["ez"], ["eq%d" % b])
+
+    def small_a():
+        ts(col("ci", 3), col("ci", 1), 1, None, ALU.bitwise_and, None, ["ri"], ["x1i"])
+        ts(col("ci", 4), col("ci", 1), 1, None, ALU.logical_shift_right, None, ["ri"], ["x2i"])
+        ms(T.rst[:], 0.0, ["rst"])
+
+    def small_b():
+        ts(cX1, col("ci", 3), float(K), cPAR, ALU.mult, ALU.add, ["x1i", "par"], ["x1"])
+        ts(col("rst", 28), cR32, 512.0, None, ALU.add, None, ["r32"], ["rst"])
+        ts(cX2, col("ci", 4), 32.0, cX1, ALU.mult, ALU.add, ["x2i", "x1"], ["x2"])
+
+    def small_c():
+        ts(T.tot0[:], T.ramp[:, 0:513:512], cR32, None, ALU.add, None, ["ramp", "r32"], ["tot0"])
+        ts(T.xl[:, 0:1], cX2, float(E - 1), None, ALU.min, None, ["x2"], ["xl"])
+
+    def sums0():
+        act(T.j32[:, 0:32], T.wn[:].indirect(T.tot0[:]), AF.Relu, WN + ["tot0"], ["j32a", "cr"], bias=cN32,
+            accum_out=cCR)
+        act(T.j32[:, 32:48], T.wn[:].indirect(T.tot0[:, 0:1]), AF.Relu, WN + ["tot0"], ["j32b", "ar"], bias=cN32,
+            accum_out=cAR)
+
+    def small_d():
+        ts(cK1, cCR, K - 512.0, None, ALU.add, None, ["cr"], ["k1c"])
+        ts(cK2, cCR, K - 512.0 - 4096.0, None, ALU.add, None, ["cr"], ["k2c"])
+        ts(cT1, cCR, cPAR, cN32, ALU.add, ALU.add, ["cr", "par", "n32"], ["t1c"])
+        ts(cR14, cR, 14.0, None, ALU.mult, None, ["r"], ["r14"])
+        ts(cCP, cT1, cAR, K - 1 - 512.0, ALU.subtract, ALU.add, ["t1c", "ar"], ["cp"])
+        ts(cJ, cR28, cT1, 240.0 - 2048.0 - (K - 1) + 512.0, ALU.subtract, ALU.add, ["r28", "t1c"], ["cj"])
+        ts(T.sg2[:], T.sg2f[:], cR14, None, ALU.add, None, ["sg2f", "r14"], ["sg2"])
+        ts(T.jc[:], T.ramp[:, 0:28], cJ, None, ALU.add, None, ["ramp", "cj"], ["jc"])
+
+    def wn_fix(h):
+        w = T.wn[:, 256 * h:256 * h + 256]
+        return lambda: act(w, w, ID, ["wn%d" % h, "r64"], ["wn%d" % h], bias=cR64)
+
+    d1 = lambda b: T.d1[:, C * b:C * b + C]
+
+    def d_out(b):
+        return lambda: act(d1(b), T["r%d" % b][:, 0:C], AF.Copy, ["r%d" % b], ["d1%d" % b])
+
+    pick, pkk = choose(1, {
+        1: [eq_q(0)],
+        2: [small_a],
+        3: [eq_q(1), eq_q(2), eq_q(3), lambda: unpack(0)],
+        4: [small_b, small_c],
+        5: [lambda: ms(T.cwf[:, 0:240], 0.0, ["cwf"])],
+        6: [lambda: tt(T.pk[:, 0:K], T.rampb[:].indirect(T.eb16[:, 0:14]), T.arep[:, 0:K], ALU.add,
+                       ["rampb", "eb16", "arep0"], ["pk0"])],
+        7: [lambda: tt(T.pk[:, K:E], T.rampb[:].indirect(T.eb16[:, 14:28]), T.arep[:, K:E], ALU.add,
+                       ["rampb", "eb16", "arep1", "arep2"], ["pk1"]),
+            lambda: quant(T.vq[:], T.vs[:], T.vt[:], ["vt"], ["vq"])],
+        8: [lambda: cp(T.src1[:], T.pk[:].indirect(T.sg1[:]), ["pk0", "pk1", "sg1"], ["src1"]), small_d],
+    }, {
+        1: [lambda: act(T.rampb[:], T.ramp[:, 0:C], ID, ["ramp"], ["rampb"], scale=1.0 / 256, bias=-95.5 / 256)],
+        2: [gat("A", T.arep[:, K:K + 128], T.ramp[:, 0:C], T.ea16[:, 14:22], ["ramp", "ea16"], ["arep1"])],
+        3: [gat("A", T.arep[:, K + 128:E], T.ramp[:, 0:C], T.ea16[:, 22:28], ["ramp", "ea16"], ["arep2"])],
+        4: [wn_fix(0)], 5: [wn_fix(1)], 6: [sums0], 7: [d_out(0)], 8: [d_out(1)],
+    })
+    d_out(2)()
+    d_out(3)()
+    cp(T.ai[:], pick, pkk, ["ai"])
+    cp(T.la[:], T.ai[:], ["ai"], ["la"])
+    tt(T.bfr[:], pick, T.ai[:], ALU.subtract, pkk + ["ai"], ["bfr"])
+    ts(T.lb[:], T.bfr[:], 256.0, 95.5, ALU.mult, ALU.add, ["bfr"], ["lb"])
+    la, lb = T.la[:, 0:14], T.lb[:, 0:14]
+
+    def w2(b, part):
+        return T.w2[:, 3 * K * b + K * part:3 * K * b + K * part + K]
+
+    def w3(b, part):
+        return T.w3[:, 2 * K * b + K * part:2 * K * b + K * part + K]
+
+    for b in range(4):
+        act(w2(b, 0), d1(b).indirect(la), AF.Copy, ["d1%d" % b, "la"], ["w2A%d" % b])
+    for b in range(4):
+        tt(T.mt1[:, b:4 * K:4], d1(b).indirect(lb), w2(b, 0), ALU.add, ["d1%d" % b, "lb", "w2A%d" % b], ["m%d" % b])
+    b1 = [gat("A", w2(b, 2), d1(b), lb, ["d1%d" % b, "lb"], ["w2B%d" % b]) for b in range(4)]
+    layer(1,
+          [gat("A", T.pw2[:, 0:K], T.p1[:], la, ["p1", "la"], ["pw2A"]), b1[0], b1[1],
+           gat("V", T.pw2[:, 2 * K:3 * K], T.p1[:], lb, ["p1", "lb"], ["pw2B"])],
+          [lambda: p_mm(1), b1[2], b1[3],
+           gat("A", T.nw2[:, 0:K], T.ramp[:, 0:C], la, ["ramp", "la"], ["nw2A"]),
+           gat("V", T.nw2[:, 2 * K:3 * K], T.ramp[:, 0:C], lb, ["ramp", "lb"], ["nw2B"])])
+    unpack(1)
+    y_mm(0)
+    put_table(1, "S", "S")
+    scores(T.pw2[:, 0:K], T.pw2[:, 2 * K:3 * K], "pw2A", "pw2B")
+
+    def mid_half(t, b, part):
+        end, keys = ((w2(b, 2 * part), ["w2%s%d" % ("AB"[part], b)]) if t == 2 else
+                     (w3(b, part), ["w3%s%d%d" % ("AB"[part], b, h) for h in range(2)]))
+        return lambda: tt(T["mid%d" % t][:, E * b + K * part:E * b + K * part + K], end, T["r%d" % b][:, 0:K],
+                          ALU.add, keys + ["r%d" % b], ["mid%d%d%d" % (t, b, part)])
+
+    def mid_slots(t):
+        m = [mid_half(t, b, part) for b in range(4) for part in range(2)]
+        return {3: m[0:1], 4: m[1:2], 5: m[2:3], 6: m[3:4], 7: m[4:6], 8: m[6:8]}
+
+    def midpoints(t, ix):
+        for b in range(4):
+            gat("AV"[b % 2], T["mt%d" % t][:, b:4 * K:4], T["mid%d" % t][:, E * b:E * b + E], ix,
+                ["mid%d%d0" % (t, b), "mid%d%d1" % (t, b), "ix%d" % t], ["m%d" % b])()
+
+    def h_out(b):
+        return lambda: act(w2(b, 1), T["r%d" % b][:, 0:K], AF.Copy, ["r%d" % b], ["w2H%d" % b])
+
+    vs = mid_slots(2)
+    vs[1] = [lambda: ms(T.cwb[:, 0:240], 0.0, ["cwb"])]
+    pick, pkk = choose(2, vs, {
+        1: [h_out(0)], 2: [h_out(1)], 3: [h_out(2)], 4: [h_out(3)],
+        5: [lambda: act(T.pw2[:, K:2 * K], T.pp[:, 0:K], AF.Copy, ["pp"], ["pw2H"])],
+        6: [lambda: y_out(0, "A", "S"), lambda: y_mm(1)],
+        7: [lambda: y_out(1, "A", "S")],
+    })
+    ts(T.ix2[:], pick, float(K), None, ALU.add, None, pkk, ["ix2"])
+    ix = T.ix2[:, 0:14]
+    midpoints(2, ix)
+
+    def end3(q, b, part, a, z):
+        win = T.w2[:, 3 * K * b + K * part:3 * K * b + K * part + E]
+        at = 2 * K * b + K * part
+        keys = ["w3%s%d%d" % ("AB"[part], b, h) for h in ((0, 1) if (a, z) == (0, 14) else (0,) if a == 0 else (1,))]
+        return gat(q, T.w3[:, at + 16 * a:at + 16 * z], win, T.ix2[:, a:z],
+                   ["w2%s%d" % ("AB"[part], b), "w2H%d" % b, "ix2"], keys)
+
+    layer(2,
+          [gat("A", T.pw3[:, 0:K], T.pw2[:, 0:E], ix, ["pw2A", "pw2H", "ix2"], ["pw3A"]), end3("A", 0, 0, 0, 14),
+           gat("V", T.pw3[:, K:E], T.pw2[:, K:3 * K], ix, ["pw2H", "pw2B", "ix2"], ["pw3B"])],
+          [lambda: p_mm(2), end3("A", 0, 1, 0, 14), end3("A", 1, 0, 0, 14), end3("A", 1, 1, 0, 14),
+           end3("V", 2, 0, 0, 14)])
+    unpack(2)
+    y_mm(2)
+    put_table(2, "S", "S")
+    scores(T.pw3[:, 0:K], T.pw3[:, K:E], "pw3A", "pw3B")
+
+    pick, pkk = choose(3, mid_slots(3), {
+        1: [end3("A", 2, 1, 0, 8)], 2: [end3("A", 2, 1, 8, 14)], 3: [end3("A", 3, 0, 0, 8)],
+        4: [end3("A", 3, 0, 8, 14)], 5: [end3("A", 3, 1, 0, 8)], 6: [end3("A", 3, 1, 8, 14)],
+        7: [lambda: y_out(2, "A", "S")],
+    })
+    gat("A", T.nw3[:, 0:K], T.nw2[:, 0:E], ix, ["nw2A", "nw2H", "ix2"], ["nw3A"])()
+    gat("A", T.nw3[:, 2 * K:3 * K], T.nw2[:, K:3 * K], ix, ["nw2H", "nw2B", "ix2"], ["nw3B"])()
+    ts(T.ix3[:], pick, float(K), None, ALU.add, None, pkk, ["ix3"])
+    ix = T.ix3[:, 0:14]
+    midpoints(3, ix)
+    layer(3,
+          [gat("A", T.elb[:, 0:E:2], T.nw3[:, 0:E], ix, ["nw3A", "nw3H", "ix3"], ["el0"]),
+           gat("V", T.elb[:, E + 1:2 * E:2], T.nw3[:, K:3 * K], ix, ["nw3H", "nw3B", "ix3"], ["el3"]),
+           lambda: store("S", T.el[:], T.elb[0:128:16, :], ["el0", "el1", "el2", "el3"])],
+          [lambda: y_mm(3)])
+    put_table(3, "S", "A")
+    y_out(3, "A", "A")
+
+    g.wait_ge(T.sem.sent, sent[0])
+    g.wait_ge(T.sem.st, stores[0])
+    for q in cnt:
+        g.wait_ge(T.sem["s" + q], cnt[q])

@@ -28,8 +28,8 @@ for _n, _c, _d in [
     ("ramp", 516, F32), ("rampb", C, F32), ("jm", E, BF), ("mask", E, BF), ("nmask", E, BF), ("wn", 1024, F32),
     ("ci", 16, I32), ("uli", 8, I32), ("cf", 32, F32), ("cst", 64, F32), ("pows", 48, F32), ("t16", 48, F32),
     ("c2", 64, F32), ("cx", 56, F32), ("win2", 64, F32), ("xw", 56, F32), ("sv", 32, F32), ("g16", 32, F32),
-    ("j16", 16, F32), ("j32", 48, F32), ("rst", 56, F32), ("jc", 28, F32), ("sg2f", 28, F32),
-    ("down", 56, F32), ("cmp", 56, F32), ("cum", 56, F32), ("sm", 8 * 28, F32),
+    ("j16", 16, F32), ("j32", 112, F32), ("pw1", 32, F32), ("rst", 28, F32), ("jc", 28, F32), ("sg2f", 28, F32),
+    ("down", 56, F32), ("cmp", 56, F32), ("cmq", 56, F32), ("cum", 56, F32), ("sm", 8 * 28, F32),
     ("ai", 16, I32), ("bfr", 16, F32),
     ("ul", 8, U16), ("ea16", 28, U16), ("eb16", 28, U16), ("sg1", 28, U16), ("sg2", 28, U16), ("xl", 2, U16),
     ("off", 2, U16), ("tot", 2, U16), ("tot0", 2, U16), ("dest", 28, U16),
@@ -134,8 +134,7 @@ def rank_program(g, core, T, topo):
         return evs
 
     def op(q, fn, rd, wr):
-        wr = list(wr) + [k for k in rd if k in BANKS]
-        need(q, deps(rd, wr))
+        need(q, deps(rd, wr) + [e for k in rd if k in BANKS for e in readers.get(k, []) if e[0] != "s" + q])
         cnt[q] += 1
         ev = ("s" + q, cnt[q])
         fn().then_inc(T.sem["s" + q], 1)
@@ -176,8 +175,8 @@ def rank_program(g, core, T, topo):
     def red(out, in_, o, rd, wr, negate=False):
         op("V", lambda: V.tensor_reduce(out, in_, AX.X, o, negate=negate), rd, wr)
 
-    def scan(out, d0, d1_, init, o0, rd, wr):
-        op("V", lambda: V.tensor_tensor_scan(out, d0, d1_, init, o0, ALU.add), rd, wr)
+    def scan(out, d0, d1_, init, o0, o1, rd, wr):
+        op("V", lambda: V.tensor_tensor_scan(out, d0, d1_, init, o0, o1), rd, wr)
 
     def act(out, in_, func, rd, wr, **kw):
         op("A", lambda: A.activation(out, in_, func, **kw), rd, wr)
@@ -219,7 +218,7 @@ def rank_program(g, core, T, topo):
     iota(T.ramp[:], [[1, 516]], 0, 0, ["ramp"])
     iota(T.jm[:], [[0, 28], [1, 16]], 0, 0, ["jm"])
     (cR, cPAR, cP4, cNP1, cSC2, cR2, cC0, cF, cCP, cR28, cR14, cJ, cX1, cX2, cR32, cN32, cR64, cCR, cAR, cK1, cK2,
-     cT1, cT2) = [col("cf", j) for j in range(23)]
+     cT0, cT2) = [col("cf", j) for j in range(23)]
     RR = T.cf[:, 24:26]
     ts(col("ci", 1), col("ci", 0), 15, None, ALU.bitwise_and, None, ["pi"], ["ri"])
     ts(col("ci", 2), col("ci", 0), 16, None, ALU.bitwise_and, None, ["pi"], ["pari"])
@@ -233,11 +232,12 @@ def rank_program(g, core, T, topo):
     cp(T.ul[:], T.uli[:], ["uli"], ["ul"])
     zero = T.cst[:, 48:64]
     for j, (key, init) in enumerate((("k14", 2.0 ** -114), ("k2", 0.5), ("kh", 2.0))):
-        scan(T.pows[:, 16 * j:16 * j + 16], T.cst[:, 16 * j:16 * j + 16], zero, init, ALU.mult,
+        scan(T.pows[:, 16 * j:16 * j + 16], T.cst[:, 16 * j:16 * j + 16], zero, init, ALU.mult, ALU.add,
              [key, "k0"], ["pow%d" % j])
-    ms(T.c2[:], 0.0, ["c2"])
     ms(T.cx[:], 0.0, ["cx"])
     ts(RR, zero[:, 0:2], cR, None, ALU.add, None, ["k0", "r"], ["rr"])
+    ms(T.pw1[:], 0.0, ["pw1"])
+    ms(T.c2[:], 0.0, ["c2"])
     ts(cC0, cR, 0.0, 2.0, ALU.is_equal, ALU.mult, ["r"], ["c0"])
     ts(cR28, cR, 28.0, None, ALU.mult, None, ["r"], ["r28"])
     ts(T.t16[:, 0:16], T.ramp[:, 0:16], cR, None, ALU.is_equal, None, ["ramp", "r"], ["m16"])
@@ -249,29 +249,29 @@ def rank_program(g, core, T, topo):
     red(cSC2, T.t16[:, 32:48], ALU.add, ["t16b"], ["sc2"], True)
     act(cF, cR, ID, ["r"], ["f"], scale=1.0 / 16, bias=1.0)
     act(cR2, cR, ID, ["r"], ["r2c"], scale=2.0)
+    act(cR32, cR, ID, ["r"], ["r32"], scale=32.0)
+    act(cN32, cR, ID, ["r"], ["n32"], scale=-32.0)
+    act(cR64, cR, ID, ["r"], ["r64"], scale=64.0)
     step = [2.0 ** -4, 2.0 ** -8, 2.0 ** -12, 2.0 ** -16, 2.0 ** -20, 2.0 ** -23]
-    cxk = []
+    cxk = ["cx", "cxd"]
     for j in range(6):
         act(col("cx", 8 * j + 1), cR, ID, ["r", "cx"], ["cxa%d" % j], scale=0.0, bias=step[j])
         if j < 4:
             sc, bi = step[j + 1] - step[j], 0.0
         elif j == 4:
-            sc, bi = 0.0, -1.5
+            sc, bi = step[5] - step[4], -step[5] / 2
         else:
             sc, bi = -step[5], step[5]
         act(T.cx[:, 8 * j + 2:8 * j + 4], RR, ID, ["rr", "cx"], ["cxb%d" % j], scale=sc, bias=bi)
         cxk += ["cxa%d" % j, "cxb%d" % j]
-    act(col("cx", 36), cR, ID, ["r", "cx"], ["cxc"], scale=step[5] - step[4], bias=-step[5] / 2)
-    act(col("cx", 48), cR, ID, ["r", "cx"], ["cxd"], scale=0.0, bias=-1.5)
-    cxk += ["cx", "cxc", "cxd"]
+    act(col("cx", 48), cR, ID, ["r", "cx"], ["cxd"], scale=0.0, bias=0.75 * step[5])
+    act(T.pw1[:, 3:32:2], T.pows[:, 1:16], ID, ["pow0", "pw1"], ["pw1a"], scale=1.0 - 2.0 ** -14)
+    act(T.pw1[:, 0:2], RR, ID, ["rr", "pw1"], ["pw1b"], scale=0.0, bias=2.0 ** -100)
     act(T.c2[:, 0:2], RR, ID, ["rr", "c2"], ["c2a"], scale=1.0 / 16, bias=1.0)
     act(T.c2[:, 32:34], RR, ID, ["rr", "c2"], ["c2b"], scale=0.0, bias=1.0)
     act(T.c2[:, 3:32:2], T.pows[:, 16:31], ID, ["pow1", "c2", "f"], ["c2c"], scale=cF)
     act(T.c2[:, 35:64:2], T.pows[:, 16:31], ID, ["pow1", "c2"], ["c2d"])
     c2k = ["c2", "c2a", "c2b", "c2c", "c2d"]
-    act(cR32, cR, ID, ["r"], ["r32"], scale=32.0)
-    act(cN32, cR, ID, ["r"], ["n32"], scale=-32.0)
-    act(cR64, cR, ID, ["r"], ["r64"], scale=64.0)
 
     need("G", [("ld_w", 32)])
     sent = [0]
@@ -345,9 +345,8 @@ def rank_program(g, core, T, topo):
 
     TINY, UP = 2.0 ** -100, 2.0 ** 30
 
-    def absz(h):
-        act(T.z[:, K * h:K * h + K], T.dz[:, K * h:K * h + K], AF.Abs, ["dz%d0" % h, "dz%d1" % h], ["z%d" % h],
-            scale=UP, bias=TINY)
+    def absz(a, b, rd, wr):
+        act(T.z[:, a:b], T.dz[:, a:b], AF.Abs, rd, wr, scale=UP, bias=TINY)
 
     quant(T.uq[:], T.us[:], T.ut[:], ["ut"], ["uq"])
     cp(T.uq2[:].bitcast(dt.uint32), T.uq[:].bitcast(dt.uint32).indirect(T.ul[:]), ["uq", "ul"], ["uq2"])
@@ -365,11 +364,12 @@ def rank_program(g, core, T, topo):
         act(T.pa1[:, 16 * a:16 * b], T.p1[:].indirect(T.ea16[:, a:b]), AF.Copy, ["p1", "ea16"], ["pa1%d" % i])
     for i, (a, b) in enumerate(cuts):
         tt(T.dz[:, 16 * a:16 * b], T.p1[:].indirect(T.eb16[:, a:b]), T.pa1[:, 16 * a:16 * b],
-           ALU.subtract, ["p1", "eb16", "pa1%d" % i], ["dz%d%d" % (i // 2, i % 2)])
-    absz(0)
-    absz(1)
+           ALU.subtract, ["p1", "eb16", "pa1%d" % i], ["dq%d" % i])
+    absz(0, K, ["dq0", "dq1"], ["z0"])
+    absz(K, 352, ["dq2"], ["z1"])
+    absz(352, E, ["dq3"], ["z2"])
     ts(T.nmask[:], T.jm[:], cR, None, ALU.not_equal, None, ["jm", "r"], ["nmask"])
-    Z = ["z0", "z1"]
+    Z = ["z0", "z1", "z2"]
     sS, sL, sLO, sGN, sAL = [col("sv", j) for j in range(5)]
     piv = lambda j: col("sv", 8 + j)
     WN = ["wn0", "wn1", "wn2", "n32"]
@@ -394,9 +394,8 @@ def rank_program(g, core, T, topo):
         count(1, T.z[:], Z + ["np1"], bias=cNP1)
         own(0)
         run(1)
-        ts(o1, sS, 0.0, cR, ALU.is_ge, ALU.mult, ["S", "r"], ["off"])
-        cp(T.g16[:, 0:16], T.pows[:, 0:16].indirect(o1), ["pow0", "off"], ["g16a"])
-        red(sL, T.g16[:, 0:16], ALU.max, ["g16a"], ["L"])
+        ts(o1, sS, 0.0, cR2, ALU.is_ge, ALU.add, ["S", "r2c"], ["off"])
+        act(T.j16[:], T.pw1[:].indirect(o1), ID, ["pw1", "pw1a", "pw1b", "off"], ["j16", "L"], accum_out=sL)
         count(2, T.z[:], Z + ["sc2", "L"], scale=cSC2, bias=sL)
         own(1)
         ts(T.win2[:], T.c2[:], sL, None, ALU.mult, None, c2k + ["L"], ["win2"])
@@ -406,23 +405,24 @@ def rank_program(g, core, T, topo):
         cp(T.g16[:, 16:32], T.win2[:, 32:64].indirect(o1), ["win2", "off"], ["g16b"])
         red(sLO, T.g16[:, 16:32], ALU.add, ["g16b"], ["lo"])
         ts(T.xw[:], T.cx[:], sLO, None, ALU.mult, None, cxk + ["lo"], ["xw"] + ["xb%d" % j for j in range(3, 9)])
-        negc, unit = col("xw", 48), col("xw", 41)
         for j in range(3, 9):
             a = 8 * (j - 3)
             pk_ = "piv%d" % j
             count(j, T.z[:] if j < 8 else T.dd[:], (Z if j < 8 else ["dd"]) + [pk_], scale=-1.0, bias=piv(j))
             if j == 4:
-                scan(T.zs[:], T.nmask[:], T.zm[:], 0.0, ALU.mult, ["nmask", "zm0", "zm1"], ["zs"])
+                scan(T.zs[:], T.nmask[:], T.zm[:], 0.0, ALU.mult, ALU.add, ["nmask", "zm0", "zm1"], ["zs"])
             if j == 5:
-                ts(T.dd[:], T.z[:], negc, None, ALU.add, None, Z + ["xw"], ["dd"])
+                ts(T.dd[:], T.z[:], piv(4), None, ALU.subtract, None, Z + ["piv4"], ["dd"])
             if j == 6:
-                ts(T.down[:, 0:28], T.zs[:, 15:E:16], negc, unit, ALU.add, ALU.add, ["zs", "xw"], ["dn0"])
-                ts(T.down[:, 28:56], T.zs[:, 15:E:16], negc, None, ALU.add, None, ["zs", "xw"], ["dn1"])
+                ts(T.down[:, 0:28], T.zs[:, 15:E:16], piv(4), col("xw", 48), ALU.subtract, ALU.add,
+                   ["zs", "xw", "piv4"], ["dn0"])
+                ts(T.down[:, 28:56], T.zs[:, 15:E:16], piv(4), None, ALU.subtract, None, ["zs", "piv4"], ["dn1"])
             if j > 3:
                 run(j)
             xb = T.xw[:, a + 2:a + 4]
             if j == 7:
-                ts(xb, xb, piv(j), col("xw", 36), ALU.add, ALU.add, ["xw", pk_], ["xb%d" % j])
+                ts(col("sv", 7), piv(7), piv(4), None, ALU.subtract, None, [pk_, "piv4"], ["p74"])
+                ts(xb, xb, col("sv", 7), None, ALU.add, None, ["xw", "p74"], ["xb%d" % j])
             else:
                 ts(xb, xb, piv(j), None, ALU.add, None, ["xw", pk_], ["xb%d" % j])
             if j == 3:
@@ -431,22 +431,28 @@ def rank_program(g, core, T, topo):
             act(T.j16[:], T.xw[:, a:a + 8].indirect(o1), ID, ["xw", "xb%d" % j, "off"], ["j16", "piv%d" % (j + 1)],
                 accum_out=piv(j + 1))
         sm = lambda j: T.sm[:, 28 * j:28 * j + 28]
-        ge, gt = T.cmp[:, 0:28], T.cmp[:, 28:56]
-        cge, cg = T.cum[:, 0:28], T.cum[:, 28:56]
-        ts(T.cmp[:], T.down[:], piv(9), None, ALU.is_gt, None, ["dn0", "dn1", "piv9"], ["cmp"])
-        scan(T.cum[:], T.rst[:], T.cmp[:], cR32, ALU.max, ["rst", "cmp", "r32"], ["cum"])
-        tt(sm(0), ge, gt, ALU.add, ["cmp"], ["sm0"])
-        cp(T.tot[:], T.cum[:, 27:56:28], ["cum"], ["tot"])
-        act(T.j32[:, 0:32], T.wn[:].indirect(T.tot[:]), AF.Relu, WN + ["tot"], ["j32a", "gn"], bias=cN32, accum_out=sGN)
-        act(T.j32[:, 32:48], T.wn[:].indirect(T.tot[:, 0:1]), AF.Relu, WN + ["tot"], ["j32b", "al"], bias=cN32,
+        ge1, gt = T.cmp[:, 0:28], T.cmp[:, 28:56]
+        ce, cg = T.cum[:, 0:28], T.cum[:, 28:56]
+        for h in range(2):
+            act(T.j32[:, 48 + 28 * h:76 + 28 * h], T.down[:, 28 * h:28 * h + 28], AF.Sign, ["dn%d" % h, "piv9"],
+                ["js%d" % h, "a%d" % h], scale=-1.0, bias=piv(9), accum_out=col("sv", 5 + h))
+        ts(T.cmq[:], T.down[:], piv(9), 1.0 / 4096, ALU.is_gt, ALU.mult, ["dn0", "dn1", "piv9"], ["cmq"])
+        ts(gt, T.down[:, 28:56], piv(9), None, ALU.is_gt, None, ["dn1", "piv9"], ["gt"])
+        ts(ge1, T.down[:, 0:28], piv(9), 1.0, ALU.is_gt, ALU.subtract, ["dn0", "piv9"], ["ge1"])
+        scan(ce, T.cmq[:, 0:28], T.cmq[:, 28:56], cK2, ALU.add, ALU.subtract, ["cmq", "k2c"], ["ce"])
+        ts(T.tot[:, 0:1], col("sv", 5), -0.5, cT0, ALU.mult, ALU.add, ["a0", "t0c"], ["tota"])
+        ts(T.tot[:, 1:2], col("sv", 6), -0.5, cT2, ALU.mult, ALU.add, ["a1", "t2c"], ["totb"])
+        act(T.j32[:, 0:32], T.wn[:].indirect(T.tot[:]), AF.Relu, WN + ["tota", "totb"], ["j32a", "gn"], bias=cN32,
+            accum_out=sGN)
+        act(T.j32[:, 32:48], T.wn[:].indirect(T.tot[:, 0:1]), AF.Relu, WN + ["tota"], ["j32b", "al"], bias=cN32,
             accum_out=sAL)
-        tt(sm(1), cg, cge, ALU.subtract, ["cum"], ["sm1"])
-        ts(sm(2), sm(0), 4096.0, cK2, ALU.mult, ALU.add, ["sm0", "k2c"], ["sm2"])
-        tt(sm(3), sm(1), sm(2), ALU.add, ["sm1", "sm2"], ["sm3"])
-        ts(sm(4), sm(1), cK1, sGN, ALU.add, ALU.max, ["sm1", "gn", "k1c"], ["sm4"])
-        ts(sm(5), sm(3), sGN, 2048.0, ALU.is_lt, ALU.mult, ["sm3", "gn"], ["sm5"])
-        tt(sm(6), cg, sm(4), ALU.subtract, ["sm4", "cum"], ["sm6"])
-        tt(sm(7), sm(5), T.jc[:], ALU.add, ["sm5", "jc"], ["sm7"])
+        tt(sm(1), ge1, gt, ALU.add, ["ge1", "gt"], ["sm1"])
+        scan(cg, gt, T.rst[:], cK1, ALU.add, ALU.add, ["gt", "rst", "k1c"], ["cg"])
+        tt(sm(3), sm(1), ce, ALU.subtract, ["sm1", "ce"], ["sm3"])
+        ts(sm(4), ce, -4096.0, sGN, ALU.mult, ALU.max, ["ce", "gn"], ["sm4"])
+        ts(sm(5), sm(3), 4096.0, sGN, ALU.mult, ALU.is_lt, ["sm3", "gn"], ["sm5"])
+        tt(sm(6), cg, sm(4), ALU.subtract, ["sm4", "cg"], ["sm6"])
+        tt(sm(7), sm(5), T.jc[:], ALU.mult, ["sm5", "jc"], ["sm7"])
         tt(sm(0), sm(6), sm(7), ALU.max, ["sm6", "sm7"], ["sm0"])
         ts(T.dest[:], sm(0), sAL, cCP, ALU.add, ALU.add, ["sm0", "al", "cp"], ["dest"])
         cw, ck, ub, src = (T.cwf, "cwf", T.uf, "src1") if t == 1 else (T.cwb, "cwb", T.ub, "src2")
@@ -473,11 +479,13 @@ def rank_program(g, core, T, topo):
         for f in after:
             f()
 
-    def scores(pa, pb, ka, kb):
-        tt(T.dz[:, 0:K], pa, T.pp[:, 0:K], ALU.subtract, [ka, "pp"], ["dz00", "dz01"])
-        tt(T.dz[:, K:E], pb, T.pp[:, 0:K], ALU.subtract, [kb, "pp"], ["dz10", "dz11"])
-        absz(0)
-        absz(1)
+    def scores(pw, at, ka, kb):
+        tt(T.dz[:, 0:K], pw[:, 0:K], T.pp[:, 0:K], ALU.subtract, [ka, "pp"], ["dq0", "dq1"])
+        tt(T.dz[:, K:352], pw[:, at:at + 128], T.pp[:, 0:128], ALU.subtract, [kb, "pp"], ["dq2"])
+        tt(T.dz[:, 352:E], pw[:, at + 128:at + K], T.pp[:, 128:K], ALU.subtract, [kb, "pp"], ["dq3"])
+        absz(0, K, ["dq0"], ["z0"])
+        absz(K, 352, ["dq2"], ["z1"])
+        absz(352, E, ["dq3"], ["z2"])
 
     def eq_q(b):
         return lambda: quant(T.eq[:, 128 * b:128 * b + 128], T.es[:, 128 * b:128 * b + 128], T.ez[:, 3 - b:515 - b],
@@ -490,11 +498,14 @@ def rank_program(g, core, T, topo):
 
     def small_b():
         ts(cX1, col("ci", 3), float(K), cPAR, ALU.mult, ALU.add, ["x1i", "par"], ["x1"])
-        ts(col("rst", 28), cR32, 512.0, None, ALU.add, None, ["r32"], ["rst"])
+        ts(cT0, cR32, 14.0, None, ALU.add, None, ["r32"], ["t0c"])
+        ts(T.tot0[:], T.ramp[:, 0:513:512], cR32, None, ALU.add, None, ["ramp", "r32"], ["tot0"])
         ts(cX2, col("ci", 4), 32.0, cX1, ALU.mult, ALU.add, ["x2i", "x1"], ["x2"])
 
     def small_c():
-        ts(T.tot0[:], T.ramp[:, 0:513:512], cR32, None, ALU.add, None, ["ramp", "r32"], ["tot0"])
+        ts(cT2, cR32, 526.0, None, ALU.add, None, ["r32"], ["t2c"])
+        ts(cJ, cR28, cPAR, 240.0 + 1025.0 - K, ALU.subtract, ALU.add, ["r28", "par"], ["cj"])
+        ts(cR14, cR, 14.0, None, ALU.mult, None, ["r"], ["r14"])
         ts(T.xl[:, 0:1], cX2, float(E - 1), None, ALU.min, None, ["x2"], ["xl"])
 
     def sums0():
@@ -504,14 +515,11 @@ def rank_program(g, core, T, topo):
             accum_out=cAR)
 
     def small_d():
-        ts(cK1, cCR, K - 512.0, None, ALU.add, None, ["cr"], ["k1c"])
-        ts(cK2, cCR, K - 512.0 - 4096.0, None, ALU.add, None, ["cr"], ["k2c"])
-        ts(cT1, cCR, cPAR, cN32, ALU.add, ALU.add, ["cr", "par", "n32"], ["t1c"])
-        ts(cR14, cR, 14.0, None, ALU.mult, None, ["r"], ["r14"])
-        ts(cCP, cT1, cAR, K - 1 - 512.0, ALU.subtract, ALU.add, ["t1c", "ar"], ["cp"])
-        ts(cJ, cR28, cT1, 240.0 - 2048.0 - (K - 1) + 512.0, ALU.subtract, ALU.add, ["r28", "t1c"], ["cj"])
         ts(T.sg2[:], T.sg2f[:], cR14, None, ALU.add, None, ["sg2f", "r14"], ["sg2"])
         ts(T.jc[:], T.ramp[:, 0:28], cJ, None, ALU.add, None, ["ramp", "cj"], ["jc"])
+        ts(cK1, cCR, 1024.0, None, ALU.add, None, ["cr"], ["k1c"])
+        ts(cK2, cCR, float(K), -1.0 / 4096, ALU.add, ALU.mult, ["cr"], ["k2c"])
+        ts(cCP, cPAR, cAR, K - 1025.0, ALU.subtract, ALU.add, ["par", "ar"], ["cp"])
 
     def wn_fix(h):
         w = T.wn[:, 256 * h:256 * h + 256]
@@ -519,33 +527,29 @@ def rank_program(g, core, T, topo):
 
     d1 = lambda b: T.d1[:, C * b:C * b + C]
 
-    def d_out(b):
-        return lambda: act(d1(b), T["r%d" % b][:, 0:C], AF.Copy, ["r%d" % b], ["d1%d" % b])
-
     pick, pkk = choose(1, {
-        1: [eq_q(0)],
         2: [small_a],
-        3: [eq_q(1), eq_q(2), eq_q(3), lambda: unpack(0)],
-        4: [small_b, small_c],
-        5: [lambda: ms(T.cwf[:, 0:240], 0.0, ["cwf"])],
+        3: [eq_q(0)],
+        4: [small_b, eq_q(1)],
+        5: [small_c, eq_q(2)],
         6: [lambda: tt(T.pk[:, 0:K], T.rampb[:].indirect(T.eb16[:, 0:14]), T.arep[:, 0:K], ALU.add,
-                       ["rampb", "eb16", "arep0"], ["pk0"])],
+                       ["rampb", "eb16", "arep0"], ["pk0"]),
+            lambda: ms(T.cwf[:, 0:240], 0.0, ["cwf"]), eq_q(3), lambda: unpack(0)],
         7: [lambda: tt(T.pk[:, K:E], T.rampb[:].indirect(T.eb16[:, 14:28]), T.arep[:, K:E], ALU.add,
-                       ["rampb", "eb16", "arep1", "arep2"], ["pk1"]),
-            lambda: quant(T.vq[:], T.vs[:], T.vt[:], ["vt"], ["vq"])],
-        8: [lambda: cp(T.src1[:], T.pk[:].indirect(T.sg1[:]), ["pk0", "pk1", "sg1"], ["src1"]), small_d],
+                       ["rampb", "eb16", "arep1", "arep2"], ["pk1"]), small_d],
+        8: [lambda: cp(T.src1[:], T.pk[:].indirect(T.sg1[:]), ["pk0", "pk1", "sg1"], ["src1"])],
     }, {
-        1: [lambda: act(T.rampb[:], T.ramp[:, 0:C], ID, ["ramp"], ["rampb"], scale=1.0 / 256, bias=-95.5 / 256)],
+        1: [lambda: act(T.rampb[:], T.ramp[:, 0:C], ID, ["ramp"], ["rampb"], scale=1.0 / 512)],
         2: [gat("A", T.arep[:, K:K + 128], T.ramp[:, 0:C], T.ea16[:, 14:22], ["ramp", "ea16"], ["arep1"])],
         3: [gat("A", T.arep[:, K + 128:E], T.ramp[:, 0:C], T.ea16[:, 22:28], ["ramp", "ea16"], ["arep2"])],
-        4: [wn_fix(0)], 5: [wn_fix(1)], 6: [sums0], 7: [d_out(0)], 8: [d_out(1)],
+        4: [wn_fix(0)], 5: [wn_fix(1)], 6: [sums0],
     })
-    d_out(2)()
-    d_out(3)()
+    for b in range(4):
+        act(d1(b), T["r%d" % b][:, 0:C], AF.Copy, ["r%d" % b], ["d1%d" % b])
+    cp(T.la[:], pick, pkk, ["la"])
     cp(T.ai[:], pick, pkk, ["ai"])
-    cp(T.la[:], T.ai[:], ["ai"], ["la"])
     tt(T.bfr[:], pick, T.ai[:], ALU.subtract, pkk + ["ai"], ["bfr"])
-    ts(T.lb[:], T.bfr[:], 256.0, 95.5, ALU.mult, ALU.add, ["bfr"], ["lb"])
+    ts(T.lb[:], T.bfr[:], 512.0, None, ALU.mult, None, ["bfr"], ["lb"])
     la, lb = T.la[:, 0:14], T.lb[:, 0:14]
 
     def w2(b, part):
@@ -563,12 +567,10 @@ def rank_program(g, core, T, topo):
           [gat("A", T.pw2[:, 0:K], T.p1[:], la, ["p1", "la"], ["pw2A"]), b1[0], b1[1],
            gat("V", T.pw2[:, 2 * K:3 * K], T.p1[:], lb, ["p1", "lb"], ["pw2B"])],
           [lambda: p_mm(1), b1[2], b1[3],
-           gat("A", T.nw2[:, 0:K], T.ramp[:, 0:C], la, ["ramp", "la"], ["nw2A"]),
            gat("V", T.nw2[:, 2 * K:3 * K], T.ramp[:, 0:C], lb, ["ramp", "lb"], ["nw2B"])])
     unpack(1)
-    y_mm(0)
     put_table(1, "S", "S")
-    scores(T.pw2[:, 0:K], T.pw2[:, 2 * K:3 * K], "pw2A", "pw2B")
+    scores(T.pw2, 2 * K, "pw2A", "pw2B")
 
     def mid_half(t, b, part):
         end, keys = ((w2(b, 2 * part), ["w2%s%d" % ("AB"[part], b)]) if t == 2 else
@@ -578,24 +580,24 @@ def rank_program(g, core, T, topo):
 
     def mid_slots(t):
         m = [mid_half(t, b, part) for b in range(4) for part in range(2)]
-        return {3: m[0:1], 4: m[1:2], 5: m[2:3], 6: m[3:4], 7: m[4:6], 8: m[6:8]}
+        return {4: m[0:1], 5: m[1:2], 6: m[2:4], 7: m[4:6], 8: m[6:8]}
 
     def midpoints(t, ix):
         for b in range(4):
             gat("AV"[b % 2], T["mt%d" % t][:, b:4 * K:4], T["mid%d" % t][:, E * b:E * b + E], ix,
                 ["mid%d%d0" % (t, b), "mid%d%d1" % (t, b), "ix%d" % t], ["m%d" % b])()
 
-    def h_out(b):
-        return lambda: act(w2(b, 1), T["r%d" % b][:, 0:K], AF.Copy, ["r%d" % b], ["w2H%d" % b])
-
     vs = mid_slots(2)
-    vs[1] = [lambda: ms(T.cwb[:, 0:240], 0.0, ["cwb"])]
-    pick, pkk = choose(2, vs, {
-        1: [h_out(0)], 2: [h_out(1)], 3: [h_out(2)], 4: [h_out(3)],
-        5: [lambda: act(T.pw2[:, K:2 * K], T.pp[:, 0:K], AF.Copy, ["pp"], ["pw2H"])],
-        6: [lambda: y_out(0, "A", "S"), lambda: y_mm(1)],
-        7: [lambda: y_out(1, "A", "S")],
-    })
+    vs[2] = [lambda: quant(T.vq[:], T.vs[:], T.vt[:], ["vt"], ["vq"]), lambda: y_mm(0)]
+    vs[3] = [lambda: ms(T.cwb[:, 0:240], 0.0, ["cwb"])]
+    pick, pkk = choose(2, vs, {})
+    y_out(0, "A", "S")
+    y_mm(1)
+    for b in range(4):
+        act(w2(b, 1), T["r%d" % b][:, 0:K], AF.Copy, ["r%d" % b], ["w2H%d" % b])
+    act(T.pw2[:, K:2 * K], T.pp[:, 0:K], AF.Copy, ["pp"], ["pw2H"])
+    y_out(1, "A", "S")
+    gat("A", T.nw2[:, 0:K], T.ramp[:, 0:C], la, ["ramp", "la"], ["nw2A"])()
     ts(T.ix2[:], pick, float(K), None, ALU.add, None, pkk, ["ix2"])
     ix = T.ix2[:, 0:14]
     midpoints(2, ix)
@@ -610,18 +612,20 @@ def rank_program(g, core, T, topo):
     layer(2,
           [gat("A", T.pw3[:, 0:K], T.pw2[:, 0:E], ix, ["pw2A", "pw2H", "ix2"], ["pw3A"]), end3("A", 0, 0, 0, 14),
            gat("V", T.pw3[:, K:E], T.pw2[:, K:3 * K], ix, ["pw2H", "pw2B", "ix2"], ["pw3B"])],
-          [lambda: p_mm(2), end3("A", 0, 1, 0, 14), end3("A", 1, 0, 0, 14), end3("A", 1, 1, 0, 14),
-           end3("V", 2, 0, 0, 14)])
+          [lambda: p_mm(2), end3("A", 0, 1, 0, 14), end3("A", 1, 0, 0, 14), end3("V", 1, 1, 0, 14)])
     unpack(2)
     y_mm(2)
     put_table(2, "S", "S")
-    scores(T.pw3[:, 0:K], T.pw3[:, K:E], "pw3A", "pw3B")
+    scores(T.pw3, K, "pw3A", "pw3B")
 
-    pick, pkk = choose(3, mid_slots(3), {
-        1: [end3("A", 2, 1, 0, 8)], 2: [end3("A", 2, 1, 8, 14)], 3: [end3("A", 3, 0, 0, 8)],
-        4: [end3("A", 3, 0, 8, 14)], 5: [end3("A", 3, 1, 0, 8)], 6: [end3("A", 3, 1, 8, 14)],
-        7: [lambda: y_out(2, "A", "S")],
+    vs = mid_slots(3)
+    vs[2] = [end3("V", 3, 1, 8, 14)]
+    vs[3] = [end3("V", 3, 1, 0, 8)]
+    pick, pkk = choose(3, vs, {
+        1: [end3("A", 2, 0, 0, 8)], 2: [end3("A", 2, 0, 8, 14)], 3: [end3("A", 2, 1, 0, 8)],
+        4: [end3("A", 2, 1, 8, 14)], 5: [end3("A", 3, 0, 0, 8)], 6: [end3("A", 3, 0, 8, 14)],
     })
+    y_out(2, "A", "S")
     gat("A", T.nw3[:, 0:K], T.nw2[:, 0:E], ix, ["nw2A", "nw2H", "ix2"], ["nw3A"])()
     gat("A", T.nw3[:, 2 * K:3 * K], T.nw2[:, K:3 * K], ix, ["nw2H", "nw2B", "ix2"], ["nw3B"])()
     ts(T.ix3[:], pick, float(K), None, ALU.add, None, pkk, ["ix3"])
@@ -633,7 +637,7 @@ def rank_program(g, core, T, topo):
            lambda: store("S", T.el[:], T.elb[0:128:16, :], ["el0", "el1", "el2", "el3"])],
           [lambda: y_mm(3)])
     put_table(3, "S", "A")
-    y_out(3, "A", "A")
+    y_out(3, "V", "A")
 
     g.wait_ge(T.sem.sent, sent[0])
     g.wait_ge(T.sem.st, stores[0])

from concourse.bass import DstId, RemoteDMATransfer
from concourse.mybir import dt, AluOpType as ALU, AxisListType as AX, ActivationFunctionType as AF

C, K, R, N = 192, 224, 3, 8
E = 2 * K
Q4, U8, BF, F32, I32, U16 = "float8_e4m3fn_x4", "uint8", "bfloat16", "float32", "int32", "uint16"
CW = 1136

SCRATCH = {}
for _n, _c, _d in [
    ("xt", 4 * C, BF), ("ut", 512, BF), ("vt", 512, BF), ("eai", 28, I32), ("ebi", 28, I32),
    ("wq", 512, Q4), ("wsc", 512, U8),
    ("lq1", 512, Q4), ("ls1", 512, U8), ("lq2", 512, Q4), ("ls2", 512, U8), ("lq3", 512, Q4), ("ls3", 512, U8),
    ("rq0", 256, Q4), ("rs0", 256, U8), ("rq1", 256, Q4), ("rs1", 256, U8),
    ("uq", 128, Q4), ("us", 128, U8), ("uq2", 128, Q4), ("us2", 128, U8), ("vq", 128, Q4), ("vs", 128, U8),
    ("tq0", C, Q4), ("ts0", C, U8), ("tq1", K, Q4), ("ts1", K, U8), ("tq2", K, Q4), ("ts2", K, U8),
    ("tq3", K, Q4), ("ts3", K, U8),
    ("mq1", K, Q4), ("ms1", K, U8), ("mq2", K, Q4), ("ms2", K, U8), ("mq3", K, Q4), ("ms3", K, U8),
    ("mt1", 4 * K, BF), ("mt2", 4 * K, BF), ("mt3", 4 * K, BF),
    ("ft1", 4 * K, BF), ("ft2", 4 * K, BF), ("ft3", 4 * K, BF),
    ("ez", 516, BF), ("eq", 512, Q4), ("es", 512, U8),
    ("d1", 4 * C, BF), ("w2", 4 * 3 * K, BF), ("w3", 4 * 2 * K, BF), ("mid2", 4 * E, BF), ("mid3", 4 * E, BF),
    ("p1", C, F32), ("pw2", 3 * K, F32), ("pw3", 2 * K, F32), ("nw2", 3 * K, F32), ("nw3", 3 * K, F32),
    ("elb", 2 * E, F32), ("ysb", C + R * K, F32),
    ("pa1", E, F32), ("dz", E, F32), ("z", E, F32), ("dd", E, F32), ("zm", E, F32), ("zs", E, F32),
    ("junk", E, BF), ("arep", E, F32), ("pk", E, F32), ("src1", E, F32), ("src2", E, BF),
    ("cwf", CW, F32), ("cwb", CW, BF), ("uf", E, F32), ("ub", E, BF),
    ("ramp", 516, F32), ("rampb", C, F32), ("jm", E, BF), ("mask", E, BF), ("nmask", E, BF), ("wn", 1024, F32),
    ("ci", 16, I32), ("uli", 8, I32), ("cf", 32, F32), ("cst", 64, F32), ("pows", 48, F32), ("t16", 48, F32),
    ("c2", 64, F32), ("cx", 56, F32), ("win2", 64, F32), ("xw", 56, F32), ("sv", 32, F32), ("g16", 32, F32),
    ("j16", 16, F32), ("j32", 112, F32), ("pw1", 32, F32), ("rst", 28, F32), ("jc", 28, F32), ("sg2f", 28, F32),
    ("down", 56, F32), ("cmp", 56, F32), ("cmq", 56, F32), ("cum", 56, F32), ("sm", 8 * 28, F32),
    ("ai", 16, I32), ("bfr", 16, F32),
    ("ul", 8, U16), ("ea16", 28, U16), ("eb16", 28, U16), ("sg1", 28, U16), ("sg2", 28, U16), ("xl", 2, U16),
    ("off", 2, U16), ("tot", 2, U16), ("tot0", 2, U16), ("dest", 28, U16),
    ("la", 16, U16), ("lb", 16, U16), ("ix2", 16, U16), ("ix3", 16, U16),
]:
    SCRATCH[_n] = ("sbuf", [128, _c], _d)
BANKS = ("r0", "r1", "r2", "r3", "pp", "py")
for _n in BANKS:
    SCRATCH[_n] = ("psum", [128, 512], F32)

SEMAPHORES = ["sV", "sA", "sP", "sG", "ld_x", "ld_u", "ld_e", "ld_w", "ld_v", "st",
              "arr1", "arr2", "arr3", "rin0", "rin1", "sent"]


def bits(engs):
    m = 0
    for e in engs:
        m |= 1 << e
    return m


def helpers(T, topo, src, dst):
    by_die = {}
    for c in topo.cores_of(src):
        if T.rank_of(c) is None and topo.may_write(c, dst) and topo.die(c) not in by_die:
            by_die[topo.die(c)] = c
    return [by_die[d] for d in sorted(by_die)]


def routes(T, topo):
    out, slot = [], {}
    for s in range(N):
        src = T.cores[s]
        slot[s] = [c for c in topo.cores_of(src) if T.rank_of(c) is not None].index(src)
        for t in range(1, R + 1):
            d = (s - t) % N
            dst = T.cores[d]
            out.append((s, t, d, None if topo.may_write(src, dst) else helpers(T, topo, src, dst)))
    return out, slot


def send_pair(g, T, topo, src, dst, oq, os_, iq, is_, sem):
    rid, pid = topo.addr(dst, src)
    m = topo.mask(src, dst)
    g.remote_dma(oq.bitcast(dt.uint8), iq.bitcast(dt.uint8), sem, T.sem.sent, pid, rid, m)
    g.remote_dma(os_, is_, sem, T.sem.sent, pid, rid, m)
    return 2 * len(topo.engines(src, dst))


def helper_program(g, core, T, topo):
    rts, slot = routes(T, topo)
    jobs = sorted((t, s, d, h.index(core)) for s, t, d, h in rts if h and core in h)
    if not jobs:
        return
    waited, sent = set(), 0
    for t, s, d, half in jobs:
        k = slot[s]
        if k not in waited:
            waited.add(k)
            g.wait_ge(T.sem["rin%d" % k], len(topo.engines(T.cores[s], core)))
        a = 256 * half
        sent += send_pair(g, T, topo, core, T.cores[d], T["lq%d" % t][:, a:a + 256], T["ls%d" % t][:, a:a + 256],
                          T["rq%d" % k][:], T["rs%d" % k][:], T.sem["arr%d" % t])
        if t == 1:
            g.wait_ge(T.sem.sent, sent)
    g.wait_ge(T.sem.sent, sent)


def rank_program(g, core, T, topo):
    rank = T.rank_of(core)
    if rank is None:
        helper_program(g, core, T, topo)
        return
    rts, slot = routes(T, topo)
    qs = {"V": g.vector, "A": g.scalar, "P": g.tensor, "G": g, "S": g.sync}
    cnt = {"V": 0, "A": 0, "P": 0, "G": 0}
    known = {q: {} for q in qs}
    snap, lastw, readers = {}, {}, {}
    stores = [0]

    def need(q, evs):
        kn = known[q]
        best = {}
        for s, v in evs:
            if v > best.get(s, 0):
                best[s] = v
        for s, v in sorted(best.items(), key=lambda sv: -len(snap.get(sv, {}))):
            if kn.get(s, 0) >= v:
                continue
            qs[q].wait_ge(T.sem[s], v)
            kn[s] = v
            for s2, v2 in snap.get((s, v), {}).items():
                if v2 > kn.get(s2, 0):
                    kn[s2] = v2

    def deps(rd, wr):
        evs = [lastw[k] for k in rd]
        for k in wr:
            if k in lastw:
                evs.append(lastw[k])
            evs.extend(readers.get(k, []))
        return evs

    def op(q, fn, rd, wr):
        need(q, deps(rd, wr) + [e for k in rd if k in BANKS for e in readers.get(k, []) if e[0] != "s" + q])
        cnt[q] += 1
        ev = ("s" + q, cnt[q])
        fn().then_inc(T.sem["s" + q], 1)
        snap[ev] = dict(known[q])
        for k in rd:
            readers.setdefault(k, []).append(ev)
        for k in wr:
            lastw[k] = ev
            readers[k] = []

    def load(q, out, in_, sem, key, total):
        qs[q].dma_start(out, in_).then_inc(T.sem[sem], 16)
        lastw[key] = (sem, total)

    def store(q, out, in_, rd):
        need(q, deps(rd, []))
        qs[q].dma_start(out, in_).then_inc(T.sem.st, 16)
        stores[0] += 16

    V, A, P = g.vector, g.scalar, g.tensor
    ID = AF.Identity

    def ts(out, in0, s1, s2, o0, o1, rd, wr):
        if o1 is None:
            op("V", lambda: V.tensor_scalar(out, in0, s1, None, o0), rd, wr)
        else:
            op("V", lambda: V.tensor_scalar(out, in0, s1, s2, o0, o1), rd, wr)

    def tt(out, in0, in1, o, rd, wr):
        op("V", lambda: V.tensor_tensor(out, in0, in1, o), rd, wr)

    def cp(out, in_, rd, wr):
        op("V", lambda: V.tensor_copy(out, in_), rd, wr)

    def ms(out, c, wr):
        op("V", lambda: V.memset(out, c), [], wr)

    def red(out, in_, o, rd, wr, negate=False):
        op("V", lambda: V.tensor_reduce(out, in_, AX.X, o, negate=negate), rd, wr)

    def scan(out, d0, d1_, init, o0, o1, rd, wr):
        op("V", lambda: V.tensor_tensor_scan(out, d0, d1_, init, o0, o1), rd, wr)

    def act(out, in_, func, rd, wr, **kw):
        op("A", lambda: A.activation(out, in_, func, **kw), rd, wr)

    def mv(q, out, in_, rd, wr):
        if q == "V":
            cp(out, in_, rd, wr)
        else:
            act(out, in_, AF.Copy, rd, wr)

    def gat(q, out, win, lst, rd, wr):
        return lambda: mv(q, out, win.indirect(lst), rd, wr)

    def quant(oq, os_, in_, rd, wr):
        op("V", lambda: V.quantize_mx(oq, os_, in_), rd, wr)

    def mm(bank, n, lq, ls, rq, rs, rd):
        op("P", lambda: P.matmul_mx(T[bank][:, 0:n], lq, ls, rq, rs, True, True), rd, [bank])

    def iota(out, pat, base, cm, wr, flt=True):
        if flt:
            op("G", lambda: g.iota(out, pat, base, cm, allow_small_or_imprecise_dtypes=True), [], wr)
        else:
            op("G", lambda: g.iota(out, pat, base, cm), [], wr)

    def col(name, j):
        return T[name][:, j:j + 1]

    load("A", T.ut[:], T.u[:], "ld_u", "ut", 16)
    load("S", T.xt[:], T.x[:], "ld_x", "xt", 16)
    load("A", T.eai[:], T.ea[:], "ld_e", "eai", 32)
    load("A", T.ebi[:], T.eb[:], "ld_e", "ebi", 32)
    load("S", T.wq[:].bitcast(dt.uint8), T.wc[:], "ld_w", "wq", 32)
    load("S", T.wsc[:], T.ws[:], "ld_w", "wsc", 32)
    load("S", T.vt[:], T.v[:], "ld_v", "vt", 16)

    iota(col("ci", 0), [[1, 1]], 0, 1, ["pi"], False)
    iota(T.uli[:], [[16, 8]], 0, 0, ["uli"], False)
    iota(T.ramp[:], [[1, 516]], 0, 0, ["ramp"])
    iota(T.jm[:], [[0, 28], [1, 16]], 0, 0, ["jm"])
    (cR, cPAR, cP4, cNP1, cSC2, cR2, cC0, cF, cCP, cR28, cR14, cJ, cX1, cX2, cR32, cN32, cR64, cCR, cAR, cK1, cK2,
     cT0, cT2) = [col("cf", j) for j in range(23)]
    RR = T.cf[:, 24:26]
    ts(col("ci", 1), col("ci", 0), 15, None, ALU.bitwise_and, None, ["pi"], ["ri"])
    ts(col("ci", 2), col("ci", 0), 16, None, ALU.bitwise_and, None, ["pi"], ["pari"])
    ts(cP4, col("ci", 0), 4.0, 3.0, ALU.mult, ALU.add, ["pi"], ["p4"])
    ms(T.cst[:, 0:16], 2.0 ** 14, ["k14"])
    ms(T.cst[:, 16:32], 2.0, ["k2"])
    ms(T.cst[:, 32:48], 0.5, ["kh"])
    ms(T.cst[:, 48:64], 0.0, ["k0"])
    cp(cR, col("ci", 1), ["ri"], ["r"])
    cp(cPAR, col("ci", 2), ["pari"], ["par"])
    cp(T.ul[:], T.uli[:], ["uli"], ["ul"])
    zero = T.cst[:, 48:64]
    for j, (key, init) in enumerate((("k14", 2.0 ** -114), ("k2", 0.5), ("kh", 2.0))):
        scan(T.pows[:, 16 * j:16 * j + 16], T.cst[:, 16 * j:16 * j + 16], zero, init, ALU.mult, ALU.add,
             [key, "k0"], ["pow%d" % j])
    ms(T.cx[:], 0.0, ["cx"])
    ts(RR, zero[:, 0:2], cR, None, ALU.add, None, ["k0", "r"], ["rr"])
    ms(T.pw1[:], 0.0, ["pw1"])
    ms(T.c2[:], 0.0, ["c2"])
    ts(cC0, cR, 0.0, 2.0, ALU.is_equal, ALU.mult, ["r"], ["c0"])
    ts(cR28, cR, 28.0, None, ALU.mult, None, ["r"], ["r28"])
    ts(T.t16[:, 0:16], T.ramp[:, 0:16], cR, None, ALU.is_equal, None, ["ramp", "r"], ["m16"])
    ts(T.sg1[:], T.ramp[:, 0:28], cR28, None, ALU.add, None, ["ramp", "r28"], ["sg1"])
    tt(T.t16[:, 16:32], T.t16[:, 0:16], T.pows[:, 0:16], ALU.mult, ["m16", "pow0"], ["t16a"])
    tt(T.t16[:, 32:48], T.t16[:, 0:16], T.pows[:, 32:48], ALU.mult, ["m16", "pow2"], ["t16b"])
    ts(T.ez[:], T.ramp[:], cP4, 0.5, ALU.is_equal, ALU.mult, ["ramp", "p4"], ["ez"])
    red(cNP1, T.t16[:, 16:32], ALU.add, ["t16a"], ["np1"], True)
    red(cSC2, T.t16[:, 32:48], ALU.add, ["t16b"], ["sc2"], True)
    act(cF, cR, ID, ["r"], ["f"], scale=1.0 / 16, bias=1.0)
    act(cR2, cR, ID, ["r"], ["r2c"], scale=2.0)
    act(cR32, cR, ID, ["r"], ["r32"], scale=32.0)
    act(cN32, cR, ID, ["r"], ["n32"], scale=-32.0)
    act(cR64, cR, ID, ["r"], ["r64"], scale=64.0)
    step = [2.0 ** -4, 2.0 ** -8, 2.0 ** -12, 2.0 ** -16, 2.0 ** -20, 2.0 ** -23]
    cxk = ["cx", "cxd"]
    for j in range(6):
        act(col("cx", 8 * j + 1), cR, ID, ["r", "cx"], ["cxa%d" % j], scale=0.0, bias=step[j])
        if j < 4:
            sc, bi = step[j + 1] - step[j], 0.0
        elif j == 4:
            sc, bi = step[5] - step[4], -step[5] / 2
        else:
            sc, bi = -step[5], step[5]
        act(T.cx[:, 8 * j + 2:8 * j + 4], RR, ID, ["rr", "cx"], ["cxb%d" % j], scale=sc, bias=bi)
        cxk += ["cxa%d" % j, "cxb%d" % j]
    act(col("cx", 48), cR, ID, ["r", "cx"], ["cxd"], scale=0.0, bias=0.75 * step[5])
    act(T.pw1[:, 3:32:2], T.pows[:, 1:16], ID, ["pow0", "pw1"], ["pw1a"], scale=1.0 - 2.0 ** -14)
    act(T.pw1[:, 0:2], RR, ID, ["rr", "pw1"], ["pw1b"], scale=0.0, bias=2.0 ** -100)
    act(T.c2[:, 0:2], RR, ID, ["rr", "c2"], ["c2a"], scale=1.0 / 16, bias=1.0)
    act(T.c2[:, 32:34], RR, ID, ["rr", "c2"], ["c2b"], scale=0.0, bias=1.0)
    act(T.c2[:, 3:32:2], T.pows[:, 16:31], ID, ["pow1", "c2", "f"], ["c2c"], scale=cF)
    act(T.c2[:, 35:64:2], T.pows[:, 16:31], ID, ["pow1", "c2"], ["c2d"])
    c2k = ["c2", "c2a", "c2b", "c2c", "c2d"]

    need("G", [("ld_w", 32)])
    sent = [0]
    late = []
    fed = False
    for t, d, h in sorted((t, d, h) for s, t, d, h in rts if s == rank):
        dst = T.cores[d]
        if h is None:
            if t == 1:
                sent[0] += send_pair(g, T, topo, core, dst, T["lq%d" % t][:], T["ls%d" % t][:], T.wq[:], T.wsc[:],
                                     T.sem["arr%d" % t])
            else:
                late.append((t, dst))
        elif not fed:
            fed = True
            k = slot[rank]
            for name, srcn, cast in (("rq%d" % k, "wq", True), ("rs%d" % k, "wsc", False)):
                trs = []
                for half, hc in enumerate(h):
                    eng = topo.engines(core, hc)
                    eng = eng[half * len(eng) // 2:(half + 1) * len(eng) // 2]
                    rid, pid = topo.addr(hc, core)
                    s_ap, d_ap = T[srcn][:, 256 * half:256 * half + 256], T[name][:]
                    if cast:
                        s_ap, d_ap = s_ap.bitcast(dt.uint8), d_ap.bitcast(dt.uint8)
                    trs.append(RemoteDMATransfer(dst_ids=[DstId(rid=rid, pnc=pid)], dma_engine_mask=bits(eng),
                                                 remote_sem=T.sem["rin%d" % k], src=s_ap, dst=d_ap))
                    sent[0] += len(eng)
                g.remote_dma_fused(trs, local_sem=T.sem.sent)
    for s, t, d, h in rts:
        if d == rank:
            lastw["l%d" % t] = ("arr%d" % t, sum(2 * len(topo.engines(c, core)) for c in (h or [T.cores[s]])))
    iota(T.wn[:, 0:512], [[-32, 16], [1, 32]], -29, 0, ["wn0", "wn1"])
    iota(T.wn[:, 512:1024], [[1, 512]], 0, 0, ["wn2"])
    iota(T.sg2f[:], [[1, 14], [K, 2]], 0, 0, ["sg2f"])
    iota(T.nw2[:, K:2 * K], [[1, K]], C, 0, ["nw2H"])
    iota(T.src2[:], [[1, 14], [K, 2], [14, 16]], -K, 0, ["src2"])
    iota(T.nw3[:, K:2 * K], [[1, K]], C + K, 0, ["nw3H"])
    iota(T.elb[:, 1:E:2], [[1, K]], C + 2 * K, 0, ["el1"])
    iota(T.elb[:, E:2 * E:2], [[1, K]], C + 2 * K, 0, ["el2"])
    for t, dst in late:
        need("G", [lastw["l%d" % (t - 1)]])
        sent[0] += send_pair(g, T, topo, core, dst, T["lq%d" % t][:], T["ls%d" % t][:], T.wq[:], T.wsc[:],
                             T.sem["arr%d" % t])

    def span(t):
        return (0, C) if t == 0 else (C + (t - 1) * K, K)

    def put_table(t, qa, qb):
        a, n = span(t)
        key = ["t%d" % t]
        store(qa, T.oc[:, 4 * a:4 * (a + n)], T["tq%d" % t][:].bitcast(dt.uint8), key)
        for k in range(4):
            store(qb if k % 2 else qa, T.osc[4 * k:4 * k + 4, a:a + n], T["ts%d" % t][32 * k:32 * k + 4, :], key)

    def y_mm(t):
        mm("py", span(t)[1], T.vq[:], T.vs[:], T["tq%d" % t][:], T["ts%d" % t][:], ["vq", "t%d" % t])

    def y_out(t, q, sq):
        a, n = span(t)
        mv(q, T.ysb[:, a:a + n], T.py[:, 0:n], ["py"], ["y%d" % t])
        store(sq, T.y[:, a:a + n], T.ysb[:, a:a + n], ["y%d" % t])

    def unpack(t):
        for b in range(4):
            mm("r%d" % b, span(t)[1], T.eq[:, 128 * b:128 * b + 128], T.es[:, 128 * b:128 * b + 128],
               T["tq%d" % t][:], T["ts%d" % t][:], ["eq%d" % b, "t%d" % t])

    def p_mm(t):
        mm("pp", span(t)[1], T.uq2[:], T.us2[:], T["tq%d" % t][:], T["ts%d" % t][:], ["uq2", "us2", "t%d" % t])

    TINY, UP = 2.0 ** -100, 2.0 ** 30

    def absz(a, b, rd, wr):
        act(T.z[:, a:b], T.dz[:, a:b], AF.Abs, rd, wr, scale=UP, bias=TINY)

    quant(T.uq[:], T.us[:], T.ut[:], ["ut"], ["uq"])
    cp(T.uq2[:].bitcast(dt.uint32), T.uq[:].bitcast(dt.uint32).indirect(T.ul[:]), ["uq", "ul"], ["uq2"])
    act(T.us2[:], T.us[:].indirect(T.ul[:]), AF.Copy, ["uq", "ul"], ["us2"])
    quant(T.tq0[:], T.ts0[:], T.xt[:], ["xt"], ["t0"])
    cp(T.ea16[:], T.eai[:], ["eai"], ["ea16"])
    cp(T.eb16[:], T.ebi[:], ["ebi"], ["eb16"])
    p_mm(0)
    put_table(0, "S", "S")
    gat("A", T.arep[:, 0:K], T.ramp[:, 0:C], T.ea16[:, 0:14], ["ramp", "ea16"], ["arep0"])()
    cp(T.p1[:], T.pp[:, 0:C], ["pp"], ["p1"])
    ts(T.mask[:], T.jm[:], cR, None, ALU.is_equal, None, ["jm", "r"], ["mask"])
    cuts = ((0, 6), (6, 14), (14, 22), (22, 28))
    for i, (a, b) in enumerate(cuts):
        act(T.pa1[:, 16 * a:16 * b], T.p1[:].indirect(T.ea16[:, a:b]), AF.Copy, ["p1", "ea16"], ["pa1%d" % i])
    for i, (a, b) in enumerate(cuts):
        tt(T.dz[:, 16 * a:16 * b], T.p1[:].indirect(T.eb16[:, a:b]), T.pa1[:, 16 * a:16 * b],
           ALU.subtract, ["p1", "eb16", "pa1%d" % i], ["dq%d" % i])
    absz(0, K, ["dq0", "dq1"], ["z0"])
    absz(K, 352, ["dq2"], ["z1"])
    absz(352, E, ["dq3"], ["z2"])
    ts(T.nmask[:], T.jm[:], cR, None, ALU.not_equal, None, ["jm", "r"], ["nmask"])
    Z = ["z0", "z1", "z2"]
    sS, sL, sLO, sGN, sAL = [col("sv", j) for j in range(5)]
    piv = lambda j: col("sv", 8 + j)
    WN = ["wn0", "wn1", "wn2", "n32"]

    def choose(t, vs, as_):
        sg, sgk = (T.sg1, "sg1") if t == 1 else (T.sg2, "sg2")

        def count(j, src, rd, **kw):
            act(T.junk[:], src, AF.Sign, rd, ["junk", "S"], accum_out=sS, **kw)
            for f in as_.get(j, []):
                f()

        def run(j):
            for f in vs.get(j, []):
                f()

        def own(h):
            tt(T.zm[:, K * h:K * h + K], T.z[:].indirect(sg[:, 14 * h:14 * h + 14]), T.mask[:, K * h:K * h + K],
               ALU.mult, Z + [sgk, "mask"], ["zm%d" % h])

        o1 = T.off[:, 0:1]
        count(1, T.z[:], Z + ["np1"], bias=cNP1)
        own(0)
        run(1)
        ts(o1, sS, 0.0, cR2, ALU.is_ge, ALU.add, ["S", "r2c"], ["off"])
        act(T.j16[:], T.pw1[:].indirect(o1), ID, ["pw1", "pw1a", "pw1b", "off"], ["j16", "L"], accum_out=sL)
        count(2, T.z[:], Z + ["sc2", "L"], scale=cSC2, bias=sL)
        own(1)
        ts(T.win2[:], T.c2[:], sL, None, ALU.mult, None, c2k + ["L"], ["win2"])
        run(2)
        ts(o1, sS, 0.0, cR2, ALU.is_le, ALU.add, ["S", "r2c"], ["off"])
        act(T.j16[:], T.win2[:, 0:32].indirect(o1), ID, ["win2", "off"], ["j16", "piv3"], accum_out=piv(3))
        cp(T.g16[:, 16:32], T.win2[:, 32:64].indirect(o1), ["win2", "off"], ["g16b"])
        red(sLO, T.g16[:, 16:32], ALU.add, ["g16b"], ["lo"])
        ts(T.xw[:], T.cx[:], sLO, None, ALU.mult, None, cxk + ["lo"], ["xw"] + ["xb%d" % j for j in range(3, 9)])
        for j in range(3, 9):
            a = 8 * (j - 3)
            pk_ = "piv%d" % j
            count(j, T.z[:] if j < 8 else T.dd[:], (Z if j < 8 else ["dd"]) + [pk_], scale=-1.0, bias=piv(j))
            if j == 4:
                scan(T.zs[:], T.nmask[:], T.zm[:], 0.0, ALU.mult, ALU.add, ["nmask", "zm0", "zm1"], ["zs"])
            if j == 5:
                ts(T.dd[:], T.z[:], piv(4), None, ALU.subtract, None, Z + ["piv4"], ["dd"])
            if j == 6:
                ts(T.down[:, 0:28], T.zs[:, 15:E:16], piv(4), col("xw", 48), ALU.subtract, ALU.add,
                   ["zs", "xw", "piv4"], ["dn0"])
                ts(T.down[:, 28:56], T.zs[:, 15:E:16], piv(4), None, ALU.subtract, None, ["zs", "piv4"], ["dn1"])
            if j > 3:
                run(j)
            xb = T.xw[:, a + 2:a + 4]
            if j == 7:
                ts(col("sv", 7), piv(7), piv(4), None, ALU.subtract, None, [pk_, "piv4"], ["p74"])
                ts(xb, xb, col("sv", 7), None, ALU.add, None, ["xw", "p74"], ["xb%d" % j])
            else:
                ts(xb, xb, piv(j), None, ALU.add, None, ["xw", pk_], ["xb%d" % j])
            if j == 3:
                run(j)
            ts(o1, sS, 0.0, cC0, ALU.is_le, ALU.add, ["S", "c0"], ["off"])
            act(T.j16[:], T.xw[:, a:a + 8].indirect(o1), ID, ["xw", "xb%d" % j, "off"], ["j16", "piv%d" % (j + 1)],
                accum_out=piv(j + 1))
        sm = lambda j: T.sm[:, 28 * j:28 * j + 28]
        ge1, gt = T.cmp[:, 0:28], T.cmp[:, 28:56]
        ce, cg = T.cum[:, 0:28], T.cum[:, 28:56]
        for h in range(2):
            act(T.j32[:, 48 + 28 * h:76 + 28 * h], T.down[:, 28 * h:28 * h + 28], AF.Sign, ["dn%d" % h, "piv9"],
                ["js%d" % h, "a%d" % h], scale=-1.0, bias=piv(9), accum_out=col("sv", 5 + h))
        ts(T.cmq[:], T.down[:], piv(9), 1.0 / 4096, ALU.is_gt, ALU.mult, ["dn0", "dn1", "piv9"], ["cmq"])
        ts(gt, T.down[:, 28:56], piv(9), None, ALU.is_gt, None, ["dn1", "piv9"], ["gt"])
        ts(ge1, T.down[:, 0:28], piv(9), 1.0, ALU.is_gt, ALU.subtract, ["dn0", "piv9"], ["ge1"])
        scan(ce, T.cmq[:, 0:28], T.cmq[:, 28:56], cK2, ALU.add, ALU.subtract, ["cmq", "k2c"], ["ce"])
        ts(T.tot[:, 0:1], col("sv", 5), -0.5, cT0, ALU.mult, ALU.add, ["a0", "t0c"], ["tota"])
        ts(T.tot[:, 1:2], col("sv", 6), -0.5, cT2, ALU.mult, ALU.add, ["a1", "t2c"], ["totb"])
        act(T.j32[:, 0:32], T.wn[:].indirect(T.tot[:]), AF.Relu, WN + ["tota", "totb"], ["j32a", "gn"], bias=cN32,
            accum_out=sGN)
        act(T.j32[:, 32:48], T.wn[:].indirect(T.tot[:, 0:1]), AF.Relu, WN + ["tota"], ["j32b", "al"], bias=cN32,
            accum_out=sAL)
        tt(sm(1), ge1, gt, ALU.add, ["ge1", "gt"], ["sm1"])
        scan(cg, gt, T.rst[:], cK1, ALU.add, ALU.add, ["gt", "rst", "k1c"], ["cg"])
        tt(sm(3), sm(1), ce, ALU.subtract, ["sm1", "ce"], ["sm3"])
        ts(sm(4), ce, -4096.0, sGN, ALU.mult, ALU.max, ["ce", "gn"], ["sm4"])
        ts(sm(5), sm(3), 4096.0, sGN, ALU.mult, ALU.is_lt, ["sm3", "gn"], ["sm5"])
        tt(sm(6), cg, sm(4), ALU.subtract, ["sm4", "cg"], ["sm6"])
        tt(sm(7), sm(5), T.jc[:], ALU.mult, ["sm5", "jc"], ["sm7"])
        tt(sm(0), sm(6), sm(7), ALU.max, ["sm6", "sm7"], ["sm0"])
        ts(T.dest[:], sm(0), sAL, cCP, ALU.add, ALU.add, ["sm0", "al", "cp"], ["dest"])
        cw, ck, ub, src = (T.cwf, "cwf", T.uf, "src1") if t == 1 else (T.cwb, "cwb", T.ub, "src2")
        cp(cw[:].indirect(T.dest[:]), T[src][:], [src, "dest"], [ck])
        for h in range(2):
            op("V", lambda: V.transpose(ub[:, K * h:K * h + K], cw[:, 16 * h:16 * h + K]), [ck], ["u%d" % h])
        return ub[:].indirect(T.xl[:, 0:1]), ["u0", "u1", "xl"]

    def layer(t, mid, after):
        quant(T["mq%d" % t][:], T["ms%d" % t][:], T["mt%d" % t][:], ["m%d" % b for b in range(4)], ["mq"])
        for b in range(4):
            mm("r%d" % b, K, T["lq%d" % t][:, 128 * b:128 * b + 128], T["ls%d" % t][:, 128 * b:128 * b + 128],
               T["mq%d" % t][:], T["ms%d" % t][:], ["l%d" % t, "mq"])
        for f in mid:
            f()
        ft = T["ft%d" % t]
        for b in range(4):
            o, i = ft[:, b:4 * K:4], T["r%d" % b][:, 0:K]
            if b % 2 == 0:
                act(o, i, AF.Copy, ["r%d" % b], ["f%d" % b], scale=0.03125)
            else:
                ts(o, i, 0.03125, None, ALU.mult, None, ["r%d" % b], ["f%d" % b])
        quant(T["tq%d" % t][:], T["ts%d" % t][:], ft[:], ["f%d" % b for b in range(4)], ["t%d" % t])
        for f in after:
            f()

    def scores(pw, at, ka, kb):
        tt(T.dz[:, 0:K], pw[:, 0:K], T.pp[:, 0:K], ALU.subtract, [ka, "pp"], ["dq0", "dq1"])
        tt(T.dz[:, K:352], pw[:, at:at + 128], T.pp[:, 0:128], ALU.subtract, [kb, "pp"], ["dq2"])
        tt(T.dz[:, 352:E], pw[:, at + 128:at + K], T.pp[:, 128:K], ALU.subtract, [kb, "pp"], ["dq3"])
        absz(0, K, ["dq0"], ["z0"])
        absz(K, 352, ["dq2"], ["z1"])
        absz(352, E, ["dq3"], ["z2"])

    def eq_q(b):
        return lambda: quant(T.eq[:, 128 * b:128 * b + 128], T.es[:, 128 * b:128 * b + 128], T.ez[:, 3 - b:515 - b],
                             ["ez"], ["eq%d" % b])

    def small_a():
        ts(col("ci", 3), col("ci", 1), 1, None, ALU.bitwise_and, None, ["ri"], ["x1i"])
        ts(col("ci", 4), col("ci", 1), 1, None, ALU.logical_shift_right, None, ["ri"], ["x2i"])
        ms(T.rst[:], 0.0, ["rst"])

    def small_b():
        ts(cX1, col("ci", 3), float(K), cPAR, ALU.mult, ALU.add, ["x1i", "par"], ["x1"])
        ts(cT0, cR32, 14.0, None, ALU.add, None, ["r32"], ["t0c"])
        ts(T.tot0[:], T.ramp[:, 0:513:512], cR32, None, ALU.add, None, ["ramp", "r32"], ["tot0"])
        ts(cX2, col("ci", 4), 32.0, cX1, ALU.mult, ALU.add, ["x2i", "x1"], ["x2"])

    def small_c():
        ts(cT2, cR32, 526.0, None, ALU.add, None, ["r32"], ["t2c"])
        ts(cJ, cR28, cPAR, 240.0 + 1025.0 - K, ALU.subtract, ALU.add, ["r28", "par"], ["cj"])
        ts(cR14, cR, 14.0, None, ALU.mult, None, ["r"], ["r14"])
        ts(T.xl[:, 0:1], cX2, float(E - 1), None, ALU.min, None, ["x2"], ["xl"])

    def sums0():
        act(T.j32[:, 0:32], T.wn[:].indirect(T.tot0[:]), AF.Relu, WN + ["tot0"], ["j32a", "cr"], bias=cN32,
            accum_out=cCR)
        act(T.j32[:, 32:48], T.wn[:].indirect(T.tot0[:, 0:1]), AF.Relu, WN + ["tot0"], ["j32b", "ar"], bias=cN32,
            accum_out=cAR)

    def small_d():
        ts(T.sg2[:], T.sg2f[:], cR14, None, ALU.add, None, ["sg2f", "r14"], ["sg2"])
        ts(T.jc[:], T.ramp[:, 0:28], cJ, None, ALU.add, None, ["ramp", "cj"], ["jc"])
        ts(cK1, cCR, 1024.0, None, ALU.add, None, ["cr"], ["k1c"])
        ts(cK2, cCR, float(K), -1.0 / 4096, ALU.add, ALU.mult, ["cr"], ["k2c"])
        ts(cCP, cPAR, cAR, K - 1025.0, ALU.subtract, ALU.add, ["par", "ar"], ["cp"])

    def wn_fix(h):
        w = T.wn[:, 256 * h:256 * h + 256]
        return lambda: act(w, w, ID, ["wn%d" % h, "r64"], ["wn%d" % h], bias=cR64)

    d1 = lambda b: T.d1[:, C * b:C * b + C]

    pick, pkk = choose(1, {
        2: [small_a],
        3: [eq_q(0)],
        4: [small_b, eq_q(1)],
        5: [small_c, eq_q(2)],
        6: [lambda: tt(T.pk[:, 0:K], T.rampb[:].indirect(T.eb16[:, 0:14]), T.arep[:, 0:K], ALU.add,
                       ["rampb", "eb16", "arep0"], ["pk0"]),
            lambda: ms(T.cwf[:, 0:240], 0.0, ["cwf"]), eq_q(3), lambda: unpack(0)],
        7: [lambda: tt(T.pk[:, K:E], T.rampb[:].indirect(T.eb16[:, 14:28]), T.arep[:, K:E], ALU.add,
                       ["rampb", "eb16", "arep1", "arep2"], ["pk1"]), small_d],
        8: [lambda: cp(T.src1[:], T.pk[:].indirect(T.sg1[:]), ["pk0", "pk1", "sg1"], ["src1"])],
    }, {
        1: [lambda: act(T.rampb[:], T.ramp[:, 0:C], ID, ["ramp"], ["rampb"], scale=1.0 / 512)],
        2: [gat("A", T.arep[:, K:K + 128], T.ramp[:, 0:C], T.ea16[:, 14:22], ["ramp", "ea16"], ["arep1"])],
        3: [gat("A", T.arep[:, K + 128:E], T.ramp[:, 0:C], T.ea16[:, 22:28], ["ramp", "ea16"], ["arep2"])],
        4: [wn_fix(0)], 5: [wn_fix(1)], 6: [sums0],
    })
    for b in range(4):
        act(d1(b), T["r%d" % b][:, 0:C], AF.Copy, ["r%d" % b], ["d1%d" % b])
    cp(T.la[:], pick, pkk, ["la"])
    cp(T.ai[:], pick, pkk, ["ai"])
    tt(T.bfr[:], pick, T.ai[:], ALU.subtract, pkk + ["ai"], ["bfr"])
    ts(T.lb[:], T.bfr[:], 512.0, None, ALU.mult, None, ["bfr"], ["lb"])
    la, lb = T.la[:, 0:14], T.lb[:, 0:14]

    def w2(b, part):
        return T.w2[:, 3 * K * b + K * part:3 * K * b + K * part + K]

    def w3(b, part):
        return T.w3[:, 2 * K * b + K * part:2 * K * b + K * part + K]

    for b in range(4):
        act(w2(b, 0), d1(b).indirect(la), AF.Copy, ["d1%d" % b, "la"], ["w2A%d" % b])
    for b in range(4):
        tt(T.mt1[:, b:4 * K:4], d1(b).indirect(lb), w2(b, 0), ALU.add, ["d1%d" % b, "lb", "w2A%d" % b], ["m%d" % b])
    b1 = [gat("A", w2(b, 2), d1(b), lb, ["d1%d" % b, "lb"], ["w2B%d" % b]) for b in range(4)]
    layer(1,
          [gat("A", T.pw2[:, 0:K], T.p1[:], la, ["p1", "la"], ["pw2A"]), b1[0], b1[1],
           gat("V", T.pw2[:, 2 * K:3 * K], T.p1[:], lb, ["p1", "lb"], ["pw2B"])],
          [lambda: p_mm(1), b1[2], b1[3],
           gat("V", T.nw2[:, 2 * K:3 * K], T.ramp[:, 0:C], lb, ["ramp", "lb"], ["nw2B"])])
    unpack(1)
    put_table(1, "S", "S")
    scores(T.pw2, 2 * K, "pw2A", "pw2B")

    def mid_half(t, b, part):
        end, keys = ((w2(b, 2 * part), ["w2%s%d" % ("AB"[part], b)]) if t == 2 else
                     (w3(b, part), ["w3%s%d%d" % ("AB"[part], b, h) for h in range(2)]))
        return lambda: tt(T["mid%d" % t][:, E * b + K * part:E * b + K * part + K], end, T["r%d" % b][:, 0:K],
                          ALU.add, keys + ["r%d" % b], ["mid%d%d%d" % (t, b, part)])

    def mid_slots(t):
        m = [mid_half(t, b, part) for b in range(4) for part in range(2)]
        return {4: m[0:1], 5: m[1:2], 6: m[2:4], 7: m[4:6], 8: m[6:8]}

    def midpoints(t, ix):
        for b in range(4):
            gat("AV"[b % 2], T["mt%d" % t][:, b:4 * K:4], T["mid%d" % t][:, E * b:E * b + E], ix,
                ["mid%d%d0" % (t, b), "mid%d%d1" % (t, b), "ix%d" % t], ["m%d" % b])()

    vs = mid_slots(2)
    vs[2] = [lambda: quant(T.vq[:], T.vs[:], T.vt[:], ["vt"], ["vq"]), lambda: y_mm(0)]
    vs[3] = [lambda: ms(T.cwb[:, 0:240], 0.0, ["cwb"])]
    pick, pkk = choose(2, vs, {})
    y_out(0, "A", "S")
    y_mm(1)
    for b in range(4):
        act(w2(b, 1), T["r%d" % b][:, 0:K], AF.Copy, ["r%d" % b], ["w2H%d" % b])
    act(T.pw2[:, K:2 * K], T.pp[:, 0:K], AF.Copy, ["pp"], ["pw2H"])
    y_out(1, "A", "S")
    gat("A", T.nw2[:, 0:K], T.ramp[:, 0:C], la, ["ramp", "la"], ["nw2A"])()
    ts(T.ix2[:], pick, float(K), None, ALU.add, None, pkk, ["ix2"])
    ix = T.ix2[:, 0:14]
    midpoints(2, ix)

    def end3(q, b, part, a, z):
        win = T.w2[:, 3 * K * b + K * part:3 * K * b + K * part + E]
        at = 2 * K * b + K * part
        keys = ["w3%s%d%d" % ("AB"[part], b, h) for h in ((0, 1) if (a, z) == (0, 14) else (0,) if a == 0 else (1,))]
        return gat(q, T.w3[:, at + 16 * a:at + 16 * z], win, T.ix2[:, a:z],
                   ["w2%s%d" % ("AB"[part], b), "w2H%d" % b, "ix2"], keys)

    layer(2,
          [gat("A", T.pw3[:, 0:K], T.pw2[:, 0:E], ix, ["pw2A", "pw2H", "ix2"], ["pw3A"]), end3("A", 0, 0, 0, 14),
           gat("V", T.pw3[:, K:E], T.pw2[:, K:3 * K], ix, ["pw2H", "pw2B", "ix2"], ["pw3B"])],
          [lambda: p_mm(2), end3("A", 0, 1, 0, 14), end3("A", 1, 0, 0, 14), end3("V", 1, 1, 0, 14)])
    unpack(2)
    y_mm(2)
    put_table(2, "S", "S")
    scores(T.pw3, K, "pw3A", "pw3B")

    vs = mid_slots(3)
    vs[2] = [end3("V", 3, 1, 8, 14)]
    vs[3] = [end3("V", 3, 1, 0, 8)]
    pick, pkk = choose(3, vs, {
        1: [end3("A", 2, 0, 0, 8)], 2: [end3("A", 2, 0, 8, 14)], 3: [end3("A", 2, 1, 0, 8)],
        4: [end3("A", 2, 1, 8, 14)], 5: [end3("A", 3, 0, 0, 8)], 6: [end3("A", 3, 0, 8, 14)],
    })
    y_out(2, "A", "S")
    gat("A", T.nw3[:, 0:K], T.nw2[:, 0:E], ix, ["nw2A", "nw2H", "ix2"], ["nw3A"])()
    gat("A", T.nw3[:, 2 * K:3 * K], T.nw2[:, K:3 * K], ix, ["nw2H", "nw2B", "ix2"], ["nw3B"])()
    ts(T.ix3[:], pick, float(K), None, ALU.add, None, pkk, ["ix3"])
    ix = T.ix3[:, 0:14]
    midpoints(3, ix)
    layer(3,
          [gat("A", T.elb[:, 0:E:2], T.nw3[:, 0:E], ix, ["nw3A", "nw3H", "ix3"], ["el0"]),
           gat("V", T.elb[:, E + 1:2 * E:2], T.nw3[:, K:3 * K], ix, ["nw3H", "nw3B", "ix3"], ["el3"]),
           lambda: store("S", T.el[:], T.elb[0:128:16, :], ["el0", "el1", "el2", "el3"])],
          [lambda: y_mm(3)])
    put_table(3, "S", "A")
    y_out(3, "V", "A")

    g.wait_ge(T.sem.sent, sent[0])
    g.wait_ge(T.sem.st, stores[0])
    for q in cnt:
        g.wait_ge(T.sem["s" + q], cnt[q])
